import numpy as np
import ml_dtypes


def mxq(x, axis, fmt="e4m3"):
    dtype, down = {"e4m3": (ml_dtypes.float8_e4m3fn, 7), "e5m2": (ml_dtypes.float8_e5m2, 14)}[fmt]
    v = np.moveaxis(np.asarray(x, np.float32).astype(ml_dtypes.bfloat16).astype(np.float64), axis, -1)
    blocks = v.reshape(v.shape[:-1] + (-1, 32))
    amax = np.abs(blocks).max(-1, keepdims=True)
    byte = np.maximum(np.where(amax > 0, np.frexp(amax)[1] - 1 + 127, 0) - down, 1)
    scale = np.exp2(byte - 127.0)
    codes = (blocks / scale).astype(np.float32).astype(dtype).astype(np.float64)
    return np.moveaxis((codes * scale).reshape(v.shape), -1, axis)


WIDE = False


def mx_kscale(k):
    if not WIDE:
        return np.ones(k)
    levels = np.array([10, -10, 5, -5, 0])
    if k % 512:
        return np.exp2(np.random.permutation(np.resize(levels, k // 32))).repeat(32)
    a = np.empty((k // 512, 16))
    for p in range(k // 512):
        a[p, :8] = np.random.permutation(np.resize(levels, 8))
        for g in range(8):
            far = levels[np.abs(levels - a[p, g]) >= 10]
            a[p, g + 8] = far[np.random.randint(len(far))]
    return np.exp2(a.ravel()).repeat(32)


def f64(x):
    return np.asarray(x).astype(np.float64)


def striped(idx):
    return np.tile(idx.reshape(-1, 16).T, (8, 1)).astype(np.uint16)


def unstriped(offs):
    return offs[:16].T.reshape(-1).astype(np.int64)


def pack_weight(w):
    k, n = w.shape
    w = f64(np.asarray(w, np.float32).astype(ml_dtypes.bfloat16)).reshape(k // 32, 32, n)
    amax = np.abs(w).max(1)
    byte = np.clip(np.where(amax > 0, np.frexp(amax)[1] - 1 + 127 - 7, 1), 1, 254)
    scaled = (w * np.exp2(127.0 - byte)[:, None, :]).reshape(k, n).astype(np.float32)
    words = np.ascontiguousarray(scaled.reshape(k // 512, 128, 4, n).transpose(0, 1, 3, 2)).astype(ml_dtypes.float8_e4m3fn).view(np.uint8)
    return words, np.ascontiguousarray(byte.astype(np.uint8).reshape(k // 512, 16, n))


def unpack_weight(words, scales):
    g, p, n, _ = words.shape
    vals = np.ascontiguousarray(words).view(ml_dtypes.float8_e4m3fn).astype(np.float64) * np.repeat(np.exp2(scales.astype(np.float64) - 127.0), 8, axis=1)[..., None]
    return vals.transpose(0, 1, 3, 2).reshape(g * 512, n)


def silu(v):
    return v / (1.0 + np.exp(-np.maximum(v, -700.0)))


K, T, D, S, V, N = 512, 1024, 8, 512, 64, 512


def setup_inputs():
    n = np.random.standard_normal
    s = mx_kscale(K)[:, None]
    packed = pack_weight(n((K, T)) * s)
    return {
        "x_words": packed[0],
        "x_scales": packed[1],
        "w": (n((K, N)) / np.sqrt(K) / s).astype(np.float32),
        "b": (0.3 * n((N, 1))).astype(np.float32),
        "offs": striped(np.random.permutation(T)[:S]),
    }


def reference(x_words, x_scales, w, b, offs):
    idx = unstriped(offs)
    xq = unpack_weight(x_words, x_scales)[:, idx]
    y = mxq(f64(w), 0, "e4m3").T @ xq
    y = silu(y + f64(b))
    return y.reshape(N, V, D).max(axis=2)

@@ -1,0 +1,135 @@
+from contextlib import ExitStack
+
+import concourse.mybir as mybir
+
+K, T, D, S, V, N = 512, 1024, 8, 512, 64, 512
+FLOPS = 2 * K * S * N
+
+F32 = mybir.dt.float32
+BF16 = mybir.dt.bfloat16
+I32 = mybir.dt.int32
+U32 = mybir.dt.uint32
+U16 = mybir.dt.uint16
+U8 = mybir.dt.uint8
+FP8X4 = mybir.dt.float8_e4m3fn_x4
+SILU = mybir.ActivationFunctionType.Silu
+P = 128
+
+
+def tile_picked_pool_lin_silu_sub_p_kernel(tc, x_words, x_scales, w, b, offs, out):
+    nc = tc.nc
+    with ExitStack() as ctx:
+        keep = ctx.enter_context(tc.tile_pool(name="keep", bufs=1))
+        psum = ctx.enter_context(tc.psum_pool(name="psum", bufs=1))
+
+        offsets = keep.tile([P, S // 16], U16, name="offsets")
+        word_table = keep.tile([P, T], I32, name="word_table", align_bytes=64)
+        scale_table = keep.tile([P, T // 4], I32, name="scale_table", align_bytes=64)
+        nc.vector.memset(scale_table[:], 0)
+        warm_in = keep.tile([P, 8], F32, name="warm_in")
+        warm_out = keep.tile([P, 8], F32, name="warm_out")
+        nc.vector.memset(warm_in[:], 0.0)
+
+        nc.sync.dma_start(word_table[:], x_words[0].rearrange("p c r -> p (c r)").bitcast(I32))
+        nc.sync.dma_start(offsets[:], offs)
+        scale_rows = x_scales[0].bitcast(I32)
+        for q in range(4):
+            nc.scalar.dma_start(scale_table[32 * q : 32 * q + 4, :], scale_rows[4 * q : 4 * q + 4, :])
+        nc.scalar.activation(warm_out[:], warm_in[:], SILU)
+
+        w_rows = w.rearrange("(p j) n -> p j n", j=4)
+        raw = {}
+        c0 = 0
+        for width in [256,256]:
+            chunk = keep.tile([P, 4, width], F32, name="w_raw%d" % c0)
+            nc.sync.dma_start(chunk[:], w_rows[:, :, c0 : c0 + width])
+            for t in range(c0 // P, (c0 + width) // P):
+                raw[t] = chunk[:, :, t * P - c0 : (t + 1) * P - c0]
+            c0 += width
+
+        bias = keep.tile([P, 4], F32, name="bias")
+        with nc.allow_non_contiguous_dma(reason="one bias value a partition and tile"):
+            nc.gpsimd.dma_start(bias[:], b.rearrange("(t p) o -> p (t o)", p=P))
+
+        words = keep.tile([P, S], U32, name="words", align_bytes=64)
+        scales = keep.tile([P, S], U8, name="scales", align_bytes=64)
+        grouped = [keep.tile([P, P, 4], BF16, name="grouped%d" % t, align_bytes=64) for t in range(4)]
+        w_codes = [keep.tile([P, P], U32, name="w_codes%d" % t, align_bytes=64) for t in range(4)]
+        w_scales = [keep.tile([P, P], U8, name="w_scales%d" % t, align_bytes=64) for t in range(4)]
+        act = [keep.tile([P, S], F32, name="act%d" % t) for t in range(4)]
+        pooled = [keep.tile([P, V], F32, name="pooled%d" % t) for t in range(4)]
+        banks = []
+
+        def gw(a, n):
+            nc.vector.tensor_copy(words[:, a : a + n], word_table[:].bitcast(U32).indirect(offsets[:, a // 16 : (a + n) // 16]))
+
+        def gs(a, n):
+            nc.vector.tensor_copy(scales[:, a : a + n], scale_table[:].bitcast(U8).indirect(offsets[:, a // 16 : (a + n) // 16]))
+
+        def il(t, eng):
+            dst = grouped[t][:].rearrange("p (c i) j -> p c j i", i=4)
+            src = raw[t].rearrange("p j (c i) -> p c j i", i=4)
+            if eng == "v":
+                nc.vector.tensor_copy(dst, src)
+            elif eng == "s":
+                nc.scalar.copy(dst, src)
+            else:
+                nc.gpsimd.tensor_scalar(dst, src, 1.0, 0.0, mybir.AluOpType.mult, mybir.AluOpType.add)
+
+        def q(t):
+            nc.vector.quantize_mx(out=w_codes[t][:].bitcast(FP8X4), scales=w_scales[t][:], in_=grouped[t][:].rearrange("p c j -> p (c j)"))
+
+        accs = {}
+
+        def mm(t, a, n):
+            name = "bank%d" % (len(banks) % 8)
+            acc = psum.tile([P, n], F32, name=name, tag=name)
+            banks.append(acc)
+            accs[(t, a)] = acc
+            nc.tensor.matmul_mx(out=acc[:], lhsT=w_codes[t][:].bitcast(FP8X4), lhsT_scale=w_scales[t][:],
+                                rhs=words[:, a : a + n].bitcast(FP8X4), rhs_scale=scales[:, a : a + n], start=True, stop=True)
+
+        def si(t, a, n):
+            nc.scalar.activation(act[t][:, a : a + n], accs[(t, a)][:], SILU, bias=bias[:, t : t + 1])
+
+        def rd(t, a, n):
+            nc.vector.tensor_reduce(pooled[t][:, a // D : (a + n) // D], act[t][:, a : a + n].rearrange("p (v d) -> p v d", d=D),
+                                    mybir.AxisListType.X, mybir.AluOpType.max)
+
+        def st(t):
+            nc.sync.dma_start(out[t * P : (t + 1) * P, :], pooled[t][:])
+
+        gw(0,256)
+        gs(0,256)
+        gw(256,256)
+        gs(256,256)
+        il(0,"s")
+        il(1,"s")
+        q(0)
+        mm(0,0,256)
+        mm(0,256,256)
+        q(1)
+        mm(1,0,512)
+        si(0,0,256)
+        si(0,256,256)
+        il(2,"v")
+        il(3,"v")
+        q(2)
+        mm(2,0,512)
+        q(3)
+        mm(3,0,256)
+        mm(3,256,256)
+        rd(0,0,256)
+        rd(0,256,256)
+        st(0)
+        si(1,0,512)
+        rd(1,0,512)
+        st(1)
+        si(2,0,512)
+        rd(2,0,512)
+        st(2)
+        si(3,0,256)
+        si(3,256,256)
+        rd(3,0,256)
+        rd(3,256,256)
+        st(3)

@@ -29,68 +29,66 @@ def tile_picked_pool_lin_silu_sub_p_kernel(tc, x_words, x_scales, w, b, offs, ou
         warm_in = keep.tile([P, 8], F32, name="warm_in")
         warm_out = keep.tile([P, 8], F32, name="warm_out")
         nc.vector.memset(warm_in[:], 0.0)
-
-        nc.sync.dma_start(word_table[:], x_words[0].rearrange("p c r -> p (c r)").bitcast(I32))
-        nc.sync.dma_start(offsets[:], offs)
-        scale_rows = x_scales[0].bitcast(I32)
-        for q in range(4):
-            nc.scalar.dma_start(scale_table[32 * q : 32 * q + 4, :], scale_rows[4 * q : 4 * q + 4, :])
         nc.scalar.activation(warm_out[:], warm_in[:], SILU)
-
+        bias = keep.tile([P, 4], F32, name="bias")
+        scale_rows = x_scales[0].bitcast(I32)
         w_rows = w.rearrange("(p j) n -> p j n", j=4)
         raw = {}
-        c0 = 0
-        for width in [256,256]:
+
+        def lx(eng):
+            eng.dma_start(word_table[:], x_words[0].rearrange("p c r -> p (c r)").bitcast(I32))
+
+        def lo():
+            nc.sync.dma_start(offsets[:], offs)
+
+        def ls(eng, q):
+            eng.dma_start(scale_table[32 * q : 32 * q + 4, :], scale_rows[4 * q : 4 * q + 4, :])
+
+        def lw(eng, c0, width):
             chunk = keep.tile([P, 4, width], F32, name="w_raw%d" % c0)
-            nc.sync.dma_start(chunk[:], w_rows[:, :, c0 : c0 + width])
+            eng.dma_start(chunk[:], w_rows[:, :, c0 : c0 + width])
             for t in range(c0 // P, (c0 + width) // P):
                 raw[t] = chunk[:, :, t * P - c0 : (t + 1) * P - c0]
-            c0 += width
 
-        bias = keep.tile([P, 4], F32, name="bias")
-        with nc.allow_non_contiguous_dma(reason="one bias value a partition and tile"):
-            nc.gpsimd.dma_start(bias[:], b.rearrange("(t p) o -> p (t o)", p=P))
+        def lb(eng):
+            with nc.allow_non_contiguous_dma(reason="one bias value a partition and tile"):
+                eng.dma_start(bias[:], b.rearrange("(t p) o -> p (t o)", p=P))
 
-        words = keep.tile([P, S], U32, name="words", align_bytes=64)
-        scales = keep.tile([P, S], U8, name="scales", align_bytes=64)
-        grouped = [keep.tile([P, P, 4], BF16, name="grouped%d" % t, align_bytes=64) for t in range(4)]
+        words, scales, grouped, accs = {}, {}, {}, {}
         w_codes = [keep.tile([P, P], U32, name="w_codes%d" % t, align_bytes=64) for t in range(4)]
         w_scales = [keep.tile([P, P], U8, name="w_scales%d" % t, align_bytes=64) for t in range(4)]
         act = [keep.tile([P, S], F32, name="act%d" % t) for t in range(4)]
         pooled = [keep.tile([P, V], F32, name="pooled%d" % t) for t in range(4)]
-        banks = []
 
-        def gw(a, n):
-            nc.vector.tensor_copy(words[:, a : a + n], word_table[:].bitcast(U32).indirect(offsets[:, a // 16 : (a + n) // 16]))
+        def gw(a, n, tag=None):
+            words[a] = keep.tile([P, n], U32, name="words%d" % a, tag=tag or "words%d" % a, align_bytes=64)
+            nc.vector.tensor_copy(words[a][:], word_table[:].bitcast(U32).indirect(offsets[:, a // 16 : (a + n) // 16]))
 
-        def gs(a, n):
-            nc.vector.tensor_copy(scales[:, a : a + n], scale_table[:].bitcast(U8).indirect(offsets[:, a // 16 : (a + n) // 16]))
+        def gs(a, n, tag=None):
+            scales[a] = keep.tile([P, n], U8, name="scales%d" % a, tag=tag or "scales%d" % a, align_bytes=64)
+            nc.vector.tensor_copy(scales[a][:], scale_table[:].bitcast(U8).indirect(offsets[:, a // 16 : (a + n) // 16]))
 
-        def il(t, eng):
+        def il(t, eng, tag=None):
+            grouped[t] = keep.tile([P, P, 4], BF16, name="grouped%d" % t, tag=tag or "grouped%d" % t, align_bytes=64)
             dst = grouped[t][:].rearrange("p (c i) j -> p c j i", i=4)
             src = raw[t].rearrange("p j (c i) -> p c j i", i=4)
             if eng == "v":
                 nc.vector.tensor_copy(dst, src)
-            elif eng == "s":
-                nc.scalar.copy(dst, src)
             else:
-                nc.gpsimd.tensor_scalar(dst, src, 1.0, 0.0, mybir.AluOpType.mult, mybir.AluOpType.add)
+                nc.scalar.copy(dst, src)
 
         def q(t):
             nc.vector.quantize_mx(out=w_codes[t][:].bitcast(FP8X4), scales=w_scales[t][:], in_=grouped[t][:].rearrange("p c j -> p (c j)"))
 
-        accs = {}
+        def mm(t, a, bank, col):
+            if col == 0:
+                accs[bank] = psum.tile([P, 512], F32, name="bank%d" % bank)
+            n = words[a].shape[1]
+            nc.tensor.matmul_mx(out=accs[bank][:, col : col + n], lhsT=w_codes[t][:].bitcast(FP8X4), lhsT_scale=w_scales[t][:],
+                                rhs=words[a][:].bitcast(FP8X4), rhs_scale=scales[a][:], start=True, stop=True)
 
-        def mm(t, a, n):
-            name = "bank%d" % (len(banks) % 8)
-            acc = psum.tile([P, n], F32, name=name, tag=name)
-            banks.append(acc)
-            accs[(t, a)] = acc
-            nc.tensor.matmul_mx(out=acc[:], lhsT=w_codes[t][:].bitcast(FP8X4), lhsT_scale=w_scales[t][:],
-                                rhs=words[:, a : a + n].bitcast(FP8X4), rhs_scale=scales[:, a : a + n], start=True, stop=True)
-
-        def si(t, a, n):
-            nc.scalar.activation(act[t][:, a : a + n], accs[(t, a)][:], SILU, bias=bias[:, t : t + 1])
+        def si(t, a, n, bank):
+            nc.scalar.activation(act[t][:, a : a + n], accs[bank][:, 0:n], SILU, bias=bias[:, t : t + 1])
 
         def rd(t, a, n):
             nc.vector.tensor_reduce(pooled[t][:, a // D : (a + n) // D], act[t][:, a : a + n].rearrange("p (v d) -> p v d", d=D),
@@ -99,37 +97,49 @@ def tile_picked_pool_lin_silu_sub_p_kernel(tc, x_words, x_scales, w, b, offs, ou
         def st(t):
             nc.sync.dma_start(out[t * P : (t + 1) * P, :], pooled[t][:])
 
+        sy, sc, gp = nc.sync, nc.scalar, nc.gpsimd
+        lx(sy)
+        lo()
+        ls(sy,0)
+        ls(sy,1)
+        ls(sy,2)
+        ls(sy,3)
+        lw(sy,0,256)
+        lw(sy,256,256)
+        lb(sy)
         gw(0,256)
         gs(0,256)
         gw(256,256)
-        gs(256,256)
         il(0,"s")
         il(1,"s")
         q(0)
-        mm(0,0,256)
-        mm(0,256,256)
+        mm(0,0,0,0)
+        gs(256,256,"grouped0")
+        mm(0,256,1,0)
         q(1)
-        mm(1,0,512)
-        si(0,0,256)
-        si(0,256,256)
-        il(2,"v")
-        il(3,"v")
+        mm(1,0,2,0)
+        mm(1,256,2,256)
+        il(2,"s")
+        il(3,"v","grouped1")
         q(2)
-        mm(2,0,512)
         q(3)
-        mm(3,0,256)
-        mm(3,256,256)
+        mm(2,0,3,0)
+        mm(2,256,3,256)
+        mm(3,0,4,0)
+        mm(3,256,5,0)
+        si(0,0,256,0)
+        si(0,256,256,1)
         rd(0,0,256)
         rd(0,256,256)
         st(0)
-        si(1,0,512)
+        si(1,0,512,2)
         rd(1,0,512)
         st(1)
-        si(2,0,512)
+        si(2,0,512,3)
         rd(2,0,512)
         st(2)
-        si(3,0,256)
-        si(3,256,256)
+        si(3,0,256,4)
+        si(3,256,256,5)
         rd(3,0,256)
         rd(3,256,256)
         st(3)

@@ -45,7 +45,7 @@ def tile_picked_pool_lin_silu_sub_p_kernel(tc, x_words, x_scales, w, b, offs, ou
             eng.dma_start(scale_table[32 * q : 32 * q + 4, :], scale_rows[4 * q : 4 * q + 4, :])
 
         def lw(eng, c0, width):
-            chunk = keep.tile([P, 4, width], F32, name="w_raw%d" % c0)
+            chunk = keep.tile([P, 4, width], F32, name="w_raw%d" % c0, align_bytes=64)
             eng.dma_start(chunk[:], w_rows[:, :, c0 : c0 + width])
             for t in range(c0 // P, (c0 + width) // P):
                 raw[t] = chunk[:, :, t * P - c0 : (t + 1) * P - c0]
@@ -57,8 +57,8 @@ def tile_picked_pool_lin_silu_sub_p_kernel(tc, x_words, x_scales, w, b, offs, ou
         words, scales, grouped, accs = {}, {}, {}, {}
         w_codes = [keep.tile([P, P], U32, name="w_codes%d" % t, align_bytes=64) for t in range(4)]
         w_scales = [keep.tile([P, P], U8, name="w_scales%d" % t, align_bytes=64) for t in range(4)]
-        act = [keep.tile([P, S], F32, name="act%d" % t) for t in range(4)]
-        pooled = [keep.tile([P, V], F32, name="pooled%d" % t) for t in range(4)]
+        act = keep.tile([P, 4, S], F32, name="act")
+        pooled = keep.tile([P, 4, V], F32, name="pooled")
 
         def gw(a, n, tag=None):
             words[a] = keep.tile([P, n], U32, name="words%d" % a, tag=tag or "words%d" % a, align_bytes=64)
@@ -80,66 +80,72 @@ def tile_picked_pool_lin_silu_sub_p_kernel(tc, x_words, x_scales, w, b, offs, ou
         def q(t):
             nc.vector.quantize_mx(out=w_codes[t][:].bitcast(FP8X4), scales=w_scales[t][:], in_=grouped[t][:].rearrange("p c j -> p (c j)"))
 
-        def mm(t, a, bank, col):
+        def mm(t, a, bank, col, lo=0, n=None):
             if col == 0:
                 accs[bank] = psum.tile([P, 512], F32, name="bank%d" % bank)
-            n = words[a].shape[1]
+            n = scales[a].shape[1]
             nc.tensor.matmul_mx(out=accs[bank][:, col : col + n], lhsT=w_codes[t][:].bitcast(FP8X4), lhsT_scale=w_scales[t][:],
-                                rhs=words[a][:].bitcast(FP8X4), rhs_scale=scales[a][:], start=True, stop=True)
+                                rhs=words[0][:, a : a + n].bitcast(FP8X4), rhs_scale=scales[a][:], start=True, stop=True)
 
         def si(t, a, n, bank):
-            nc.scalar.activation(act[t][:, a : a + n], accs[bank][:, 0:n], SILU, bias=bias[:, t : t + 1])
+            nc.scalar.activation(act[:, t, a : a + n], accs[bank][:, 0:n], SILU, bias=bias[:, t : t + 1])
 
-        def rd(t, a, n):
-            nc.vector.tensor_reduce(pooled[t][:, a // D : (a + n) // D], act[t][:, a : a + n].rearrange("p (v d) -> p v d", d=D),
+        def rd(t, a, n, nt=1):
+            nc.vector.tensor_reduce(pooled[:, t : t + nt, a // D : (a + n) // D], act[:, t : t + nt, a : a + n].rearrange("p t (v d) -> p t v d", d=D),
                                     mybir.AxisListType.X, mybir.AluOpType.max)
 
-        def st(t):
-            nc.sync.dma_start(out[t * P : (t + 1) * P, :], pooled[t][:])
+        def st(t, nt=1):
+            nc.sync.dma_start(out.rearrange("(t p) v -> p t v", p=P)[:, t : t + nt, :], pooled[:, t : t + nt, :])
+
+        def probe(ap, k):
+            pr = keep.tile([P, 1], F32, name="probe%d" % k)
+            nc.gpsimd.tensor_copy(pr[:], ap)
 
         sy, sc, gp = nc.sync, nc.scalar, nc.gpsimd
-        lx(sy)
         lo()
+        lx(sy)
         ls(sy,0)
         ls(sy,1)
         ls(sy,2)
         ls(sy,3)
-        lw(sy,0,256)
-        lw(sy,256,256)
+        lw(sy,0,128)
+        lw(sy,128,128)
+        lw(sy,256,128)
+        lw(sy,384,128)
         lb(sy)
-        gw(0,256)
+        gw(0,512)
         gs(0,256)
-        gw(256,256)
         il(0,"s")
         il(1,"s")
+        il(2,"s")
         q(0)
         mm(0,0,0,0)
-        gs(256,256,"grouped0")
-        mm(0,256,1,0)
         q(1)
-        mm(1,0,2,0)
-        mm(1,256,2,256)
-        il(2,"s")
-        il(3,"v","grouped1")
+        mm(1,0,1,0)
+        gs(256,256,"w_raw128")
+        mm(0,256,2,0)
+        mm(1,256,3,0)
+        il(3,"v","w_raw256")
         q(2)
         q(3)
-        mm(2,0,3,0)
-        mm(2,256,3,256)
-        mm(3,0,4,0)
-        mm(3,256,5,0)
+        mm(2,0,4,0)
+        mm(2,256,5,0)
+        mm(3,0,6,0)
+        mm(3,256,7,0)
         si(0,0,256,0)
-        si(0,256,256,1)
-        rd(0,0,256)
-        rd(0,256,256)
-        st(0)
-        si(1,0,512,2)
-        rd(1,0,512)
-        st(1)
-        si(2,0,512,3)
-        rd(2,0,512)
+        si(1,0,256,1)
+        rd(0,0,256,2)
+        si(0,256,256,2)
+        si(1,256,256,3)
+        rd(0,256,256,2)
+        st(0,2)
+        si(2,0,256,4)
+        si(2,256,256,5)
+        rd(2,0,256)
+        rd(2,256,256)
         st(2)
-        si(3,0,256,4)
-        si(3,256,256,5)
+        si(3,0,256,6)
+        si(3,256,256,7)
         rd(3,0,256)
         rd(3,256,256)
         st(3)

@@ -68,14 +68,17 @@ def tile_picked_pool_lin_silu_sub_p_kernel(tc, x_words, x_scales, w, b, offs, ou
             scales[a] = keep.tile([P, n], U8, name="scales%d" % a, tag=tag or "scales%d" % a, align_bytes=64)
             nc.vector.tensor_copy(scales[a][:], scale_table[:].bitcast(U8).indirect(offsets[:, a // 16 : (a + n) // 16]))
 
-        def il(t, eng, tag=None):
-            grouped[t] = keep.tile([P, P, 4], BF16, name="grouped%d" % t, tag=tag or "grouped%d" % t, align_bytes=64)
-            dst = grouped[t][:].rearrange("p (c i) j -> p c j i", i=4)
-            src = raw[t].rearrange("p j (c i) -> p c j i", i=4)
+        def il(t, eng, lo=0, hi=P):
+            if t not in grouped:
+                grouped[t] = keep.tile([P, P, 4], BF16, name="grouped%d" % t, align_bytes=64)
+            dst = grouped[t][:, lo:hi, :].rearrange("p (c i) j -> p c j i", i=4)
+            src = raw[t][:, :, lo:hi].rearrange("p j (c i) -> p c j i", i=4)
             if eng == "v":
                 nc.vector.tensor_copy(dst, src)
-            else:
+            elif eng == "s":
                 nc.scalar.copy(dst, src)
+            else:
+                nc.gpsimd.tensor_scalar(dst, src, 1.0, 0.0, mybir.AluOpType.mult, mybir.AluOpType.add)
 
         def q(t):
             nc.vector.quantize_mx(out=w_codes[t][:].bitcast(FP8X4), scales=w_scales[t][:], in_=grouped[t][:].rearrange("p c j -> p (c j)"))
@@ -125,7 +128,8 @@ def tile_picked_pool_lin_silu_sub_p_kernel(tc, x_words, x_scales, w, b, offs, ou
         gs(256,256,"w_raw128")
         mm(0,256,2,0)
         mm(1,256,3,0)
-        il(3,"v","w_raw256")
+        il(3,"s",0,64)
+        il(3,"g",64,128)
         q(2)
         q(3)
         mm(2,0,4,0)
@@ -133,11 +137,13 @@ def tile_picked_pool_lin_silu_sub_p_kernel(tc, x_words, x_scales, w, b, offs, ou
         mm(3,0,6,0)
         mm(3,256,7,0)
         si(0,0,256,0)
+        rd(0,0,256)
         si(1,0,256,1)
-        rd(0,0,256,2)
+        rd(1,0,256)
         si(0,256,256,2)
+        rd(0,256,256)
         si(1,256,256,3)
-        rd(0,256,256,2)
+        rd(1,256,256)
         st(0,2)
         si(2,0,256,4)
         si(2,256,256,5)

@@ -1,6 +1,7 @@
 from contextlib import ExitStack
 
 import concourse.mybir as mybir
+from concourse.masks import make_identity
 
 K, T, D, S, V, N = 512, 1024, 8, 512, 64, 512
 FLOPS = 2 * K * S * N
@@ -13,6 +14,7 @@ U16 = mybir.dt.uint16
 U8 = mybir.dt.uint8
 FP8X4 = mybir.dt.float8_e4m3fn_x4
 SILU = mybir.ActivationFunctionType.Silu
+MAX = mybir.AluOpType.max
 P = 128
 
 
@@ -21,19 +23,24 @@ def tile_picked_pool_lin_silu_sub_p_kernel(tc, x_words, x_scales, w, b, offs, ou
     with ExitStack() as ctx:
         keep = ctx.enter_context(tc.tile_pool(name="keep", bufs=1))
         psum = ctx.enter_context(tc.psum_pool(name="psum", bufs=1))
+        shared = ctx.enter_context(tc.tile_pool(name="shared", bufs=1))
 
         offsets = keep.tile([P, S // 16], U16, name="offsets")
         word_table = keep.tile([P, T], I32, name="word_table", align_bytes=64)
         scale_table = keep.tile([P, T // 4], I32, name="scale_table", align_bytes=64)
-        nc.vector.memset(scale_table[:], 0)
         warm_in = keep.tile([P, 8], F32, name="warm_in")
         warm_out = keep.tile([P, 8], F32, name="warm_out")
-        nc.vector.memset(warm_in[:], 0.0)
-        nc.scalar.activation(warm_out[:], warm_in[:], SILU)
         bias = keep.tile([P, 4], F32, name="bias")
         scale_rows = x_scales[0].bitcast(I32)
         w_rows = w.rearrange("(p j) n -> p j n", j=4)
         raw = {}
+
+        def ms(eng):
+            eng.memset(scale_table[:], 0)
+
+        def warm(eng):
+            eng.memset(warm_in[:], 0.0)
+            nc.scalar.activation(warm_out[:], warm_in[:], SILU)
 
         def lx(eng):
             eng.dma_start(word_table[:], x_words[0].rearrange("p c r -> p (c r)").bitcast(I32))
@@ -44,8 +51,14 @@ def tile_picked_pool_lin_silu_sub_p_kernel(tc, x_words, x_scales, w, b, offs, ou
         def ls(eng, q):
             eng.dma_start(scale_table[32 * q : 32 * q + 4, :], scale_rows[4 * q : 4 * q + 4, :])
 
+        def lsr(eng, q):
+            eng.dma_start(scale_table[32 * q : 32 * q + 32, :], scale_rows[4 * q : 4 * q + 4, :].partition_broadcast(8))
+
         def lw(eng, c0, width):
-            chunk = keep.tile([P, 4, width], F32, name="w_raw%d" % c0, align_bytes=64)
+            if c0 + width == N:
+                chunk = shared.tile([P, 4, width], F32, name="w_raw%d" % c0, align_bytes=64, offset=1024)
+            else:
+                chunk = keep.tile([P, 4, width], F32, name="w_raw%d" % c0, align_bytes=64)
             eng.dma_start(chunk[:], w_rows[:, :, c0 : c0 + width])
             for t in range(c0 // P, (c0 + width) // P):
                 raw[t] = chunk[:, :, t * P - c0 : (t + 1) * P - c0]
@@ -54,23 +67,41 @@ def tile_picked_pool_lin_silu_sub_p_kernel(tc, x_words, x_scales, w, b, offs, ou
             with nc.allow_non_contiguous_dma(reason="one bias value a partition and tile"):
                 eng.dma_start(bias[:], b.rearrange("(t p) o -> p (t o)", p=P))
 
+        segments = keep.tile([P, 32], F32, name="segments", align_bytes=64)
+        turned = keep.tile([P, 32], F32, name="turned", align_bytes=64)
+
+        def lbv(eng):
+            nc.vector.memset(segments[:], 0.0)
+            eng.dma_start(segments[0:P:8, :], b.rearrange("(t q j) o -> q t (j o)", t=4, q=4))
+
+        def turn():
+            nc.vector.transpose(turned[:], segments[:])
+
         words, scales, grouped, accs = {}, {}, {}, {}
         w_codes = [keep.tile([P, P], U32, name="w_codes%d" % t, align_bytes=64) for t in range(4)]
         w_scales = [keep.tile([P, P], U8, name="w_scales%d" % t, align_bytes=64) for t in range(4)]
-        act = keep.tile([P, 4, S], F32, name="act")
+        act = {}
         pooled = keep.tile([P, 4, V], F32, name="pooled")
 
         def gw(a, n, tag=None):
             words[a] = keep.tile([P, n], U32, name="words%d" % a, tag=tag or "words%d" % a, align_bytes=64)
             nc.vector.tensor_copy(words[a][:], word_table[:].bitcast(U32).indirect(offsets[:, a // 16 : (a + n) // 16]))
 
+
+        def gw2(a, n):
+            nc.vector.tensor_copy(words[0][:, a : a + n], word_table[:].bitcast(U32).indirect(offsets[:, a // 16 : (a + n) // 16]))
+
         def gs(a, n, tag=None):
             scales[a] = keep.tile([P, n], U8, name="scales%d" % a, tag=tag or "scales%d" % a, align_bytes=64)
             nc.vector.tensor_copy(scales[a][:], scale_table[:].bitcast(U8).indirect(offsets[:, a // 16 : (a + n) // 16]))
 
-        def il(t, eng, lo=0, hi=P):
+        def part(table, a, n):
+            a0 = max(k for k in table if k <= a)
+            return table[a0][:, a - a0 : a - a0 + n]
+
+        def il(t, eng, lo=0, hi=P, tag=None):
             if t not in grouped:
-                grouped[t] = keep.tile([P, P, 4], BF16, name="grouped%d" % t, align_bytes=64)
+                grouped[t] = keep.tile([P, P, 4], BF16, name="grouped%d" % t, tag=tag or "grouped%d" % t, align_bytes=64)
             dst = grouped[t][:, lo:hi, :].rearrange("p (c i) j -> p c j i", i=4)
             src = raw[t][:, :, lo:hi].rearrange("p j (c i) -> p c j i", i=4)
             if eng == "v":
@@ -83,59 +114,78 @@ def tile_picked_pool_lin_silu_sub_p_kernel(tc, x_words, x_scales, w, b, offs, ou
         def q(t):
             nc.vector.quantize_mx(out=w_codes[t][:].bitcast(FP8X4), scales=w_scales[t][:], in_=grouped[t][:].rearrange("p c j -> p (c j)"))
 
-        def mm(t, a, bank, col, lo=0, n=None):
+        def mm(t, a, n, bank, col=0):
             if col == 0:
-                accs[bank] = psum.tile([P, 512], F32, name="bank%d" % bank)
-            n = scales[a].shape[1]
+                accs[bank] = psum.tile([P, 512], F32, name="acc%d_%d" % (t, a), tag="bank%d" % bank)
             nc.tensor.matmul_mx(out=accs[bank][:, col : col + n], lhsT=w_codes[t][:].bitcast(FP8X4), lhsT_scale=w_scales[t][:],
-                                rhs=words[0][:, a : a + n].bitcast(FP8X4), rhs_scale=scales[a][:], start=True, stop=True)
+                                rhs=part(words, a, n).bitcast(FP8X4), rhs_scale=part(scales, a, n), start=True, stop=True)
 
-        def si(t, a, n, bank):
-            nc.scalar.activation(act[:, t, a : a + n], accs[bank][:, 0:n], SILU, bias=bias[:, t : t + 1])
+        def place(t, a, n, offset):
+            late = shared.tile([P, n], F32, name="late%d_%d" % (t, a), align_bytes=64, offset=offset)
+            for a0 in range(0, n, 256):
+                act[t, a + a0] = late[:, a0 : a0 + 256]
 
-        def rd(t, a, n, nt=1):
-            nc.vector.tensor_reduce(pooled[:, t : t + nt, a // D : (a + n) // D], act[:, t : t + nt, a : a + n].rearrange("p t (v d) -> p t v d", d=D),
-                                    mybir.AxisListType.X, mybir.AluOpType.max)
+        def si(t, a, n, bank, tag=None):
+            if (t, a) not in act:
+                act[t, a] = keep.tile([P, n], F32, name="act%d_%d" % (t, a), tag=tag or "act%d_%d" % (t, a), align_bytes=64)[:]
+            nc.scalar.activation(act[t, a], accs[bank][:, 0:n], SILU, bias=bias[:, t : t + 1])
 
-        def st(t, nt=1):
-            nc.sync.dma_start(out.rearrange("(t p) v -> p t v", p=P)[:, t : t + nt, :], pooled[:, t : t + nt, :])
+        def rd(t, a, n):
+            nc.vector.tensor_reduce(pooled[:, t, a // D : (a + n) // D], act[t, a].rearrange("p (v d) -> p v d", d=D), mybir.AxisListType.X, MAX)
+
+        def unit(t, a, n, bank, tag=None):
+            mm(t, a, n, bank)
+            si(t, a, n, bank, tag)
+            rd(t, a, n)
+
+        def unit2(t, bank, tag=None):
+            mm(t, 0, 256, bank)
+            mm(t, 256, 256, bank, 256)
+            si(t, 0, 512, bank, tag)
+            rd(t, 0, 512)
+
+        def st(t, nt=1, eng=nc.sync):
+            eng.dma_start(out.rearrange("(t p) v -> p t v", p=P)[:, t : t + nt, :], pooled[:, t : t + nt, :])
 
         def probe(ap, k):
-            pr = keep.tile([P, 1], F32, name="probe%d" % k)
+            pr = keep.tile([P, 1], ap.dtype, name="probe%d" % k)
             nc.gpsimd.tensor_copy(pr[:], ap)
 
-        sy, sc, gp = nc.sync, nc.scalar, nc.gpsimd
+        sy, sc, gp, ve = nc.sync, nc.scalar, nc.gpsimd, nc.vector
+        ms(ve)
         lo()
         lx(sy)
+        ls(sc,2)
+        ls(sc,3)
+        warm(ve)
         ls(sy,0)
         ls(sy,1)
-        ls(sy,2)
-        ls(sy,3)
         lw(sy,0,128)
         lw(sy,128,128)
         lw(sy,256,128)
         lw(sy,384,128)
         lb(sy)
+
         gw(0,512)
         gs(0,256)
         il(0,"s")
         il(1,"s")
         il(2,"s")
         q(0)
-        mm(0,0,0,0)
+        mm(0,0,256,0)
         q(1)
-        mm(1,0,1,0)
+        mm(1,0,256,1)
         gs(256,256,"w_raw128")
-        mm(0,256,2,0)
-        mm(1,256,3,0)
+        mm(0,256,256,2)
+        mm(1,256,256,3)
         il(3,"s",0,64)
         il(3,"g",64,128)
         q(2)
         q(3)
-        mm(2,0,4,0)
-        mm(2,256,5,0)
-        mm(3,0,6,0)
-        mm(3,256,7,0)
+        mm(2,0,256,4)
+        mm(2,256,256,5)
+        mm(3,0,256,6)
+        mm(3,256,256,7)
         si(0,0,256,0)
         rd(0,0,256)
         si(1,0,256,1)

@@ -63,9 +63,14 @@ def tile_picked_pool_lin_silu_sub_p_kernel(tc, x_words, x_scales, w, b, offs, ou
             for t in range(c0 // P, (c0 + width) // P):
                 raw[t] = chunk[:, :, t * P - c0 : (t + 1) * P - c0]
 
+        bias_first = keep.tile([P, 2], F32, name="bias_first")
+        bias_rest = keep.tile([P, 2], F32, name="bias_rest")
+
         def lb(eng):
+            columns = b.rearrange("(t p) o -> p (t o)", p=P)
             with nc.allow_non_contiguous_dma(reason="one bias value a partition and tile"):
-                eng.dma_start(bias[:], b.rearrange("(t p) o -> p (t o)", p=P))
+                eng.dma_start(bias_first[:], columns[:, 0:2])
+                eng.dma_start(bias_rest[:], columns[:, 2:4])
 
         segments = keep.tile([P, 32], F32, name="segments", align_bytes=64)
         turned = keep.tile([P, 32], F32, name="turned", align_bytes=64)
@@ -125,10 +130,10 @@ def tile_picked_pool_lin_silu_sub_p_kernel(tc, x_words, x_scales, w, b, offs, ou
             for a0 in range(0, n, 256):
                 act[t, a + a0] = late[:, a0 : a0 + 256]
 
-        def si(t, a, n, bank, tag=None):
+        def si(t, a, n, bank, tag=None, col=0):
             if (t, a) not in act:
                 act[t, a] = keep.tile([P, n], F32, name="act%d_%d" % (t, a), tag=tag or "act%d_%d" % (t, a), align_bytes=64)[:]
-            nc.scalar.activation(act[t, a], accs[bank][:, 0:n], SILU, bias=bias[:, t : t + 1])
+            nc.scalar.activation(act[t, a], accs[bank][:, col : col + n], SILU, bias=bias_first[:, t : t + 1] if t < 2 else bias_rest[:, t - 2 : t - 1])
 
         def rd(t, a, n):
             nc.vector.tensor_reduce(pooled[:, t, a // D : (a + n) // D], act[t, a].rearrange("p (v d) -> p v d", d=D), mybir.AxisListType.X, MAX)
@@ -201,7 +206,9 @@ def tile_picked_pool_lin_silu_sub_p_kernel(tc, x_words, x_scales, w, b, offs, ou
         rd(2,256,256)
         st(2)
         si(3,0,256,6)
-        si(3,256,256,7)
+        si(3,256,128,7)
+        si(3,384,128,7,None,128)
         rd(3,0,256)
-        rd(3,256,256)
+        rd(3,256,128)
+        rd(3,384,128)
         st(3)

@@ -1,7 +1,6 @@
 from contextlib import ExitStack
 
 import concourse.mybir as mybir
-from concourse.masks import make_identity
 
 K, T, D, S, V, N = 512, 1024, 8, 512, 64, 512
 FLOPS = 2 * K * S * N
@@ -15,6 +14,8 @@ U8 = mybir.dt.uint8
 FP8X4 = mybir.dt.float8_e4m3fn_x4
 SILU = mybir.ActivationFunctionType.Silu
 MAX = mybir.AluOpType.max
+MULT = mybir.AluOpType.mult
+ADD = mybir.AluOpType.add
 P = 128
 
 
@@ -23,22 +24,20 @@ def tile_picked_pool_lin_silu_sub_p_kernel(tc, x_words, x_scales, w, b, offs, ou
     with ExitStack() as ctx:
         keep = ctx.enter_context(tc.tile_pool(name="keep", bufs=1))
         psum = ctx.enter_context(tc.psum_pool(name="psum", bufs=1))
-        shared = ctx.enter_context(tc.tile_pool(name="shared", bufs=1))
 
         offsets = keep.tile([P, S // 16], U16, name="offsets")
-        word_table = keep.tile([P, T], I32, name="word_table", align_bytes=64)
-        scale_table = keep.tile([P, T // 4], I32, name="scale_table", align_bytes=64)
-        warm_in = keep.tile([P, 8], F32, name="warm_in")
-        warm_out = keep.tile([P, 8], F32, name="warm_out")
-        bias = keep.tile([P, 4], F32, name="bias")
+        word_table = keep.tile([P, T], I32, name="word_table", align_bytes=256)
+        scale_table = keep.tile([P, T // 4], I32, name="scale_table", tag="scale_table", align_bytes=256)
         scale_rows = x_scales[0].bitcast(I32)
         w_rows = w.rearrange("(p j) n -> p j n", j=4)
-        raw = {}
+        raw, bias = {}, {}
 
-        def ms(eng):
-            eng.memset(scale_table[:], 0)
+        def ms(eng, lo=0, hi=T // 4):
+            eng.memset(scale_table[:, lo:hi], 0)
 
         def warm(eng):
+            warm_in = keep.tile([P, 8], F32, name="warm_in")
+            warm_out = keep.tile([P, 8], F32, name="warm_out")
             eng.memset(warm_in[:], 0.0)
             nc.scalar.activation(warm_out[:], warm_in[:], SILU)
 
@@ -54,107 +53,135 @@ def tile_picked_pool_lin_silu_sub_p_kernel(tc, x_words, x_scales, w, b, offs, ou
         def lsr(eng, q):
             eng.dma_start(scale_table[32 * q : 32 * q + 32, :], scale_rows[4 * q : 4 * q + 4, :].partition_broadcast(8))
 
-        def lw(eng, c0, width):
-            if c0 + width == N:
-                chunk = shared.tile([P, 4, width], F32, name="w_raw%d" % c0, align_bytes=64, offset=1024)
-            else:
-                chunk = keep.tile([P, 4, width], F32, name="w_raw%d" % c0, align_bytes=64)
+        def lw(eng, c0, width, tag=None):
+            chunk = keep.tile([P, 4, width], F32, name="w_raw%d" % c0, tag=tag or "w_raw%d" % c0, align_bytes=256)
             eng.dma_start(chunk[:], w_rows[:, :, c0 : c0 + width])
-            for t in range(c0 // P, (c0 + width) // P):
-                raw[t] = chunk[:, :, t * P - c0 : (t + 1) * P - c0]
+            for c in range(c0, c0 + width, 32):
+                raw[c] = (chunk, c0)
 
-        bias_first = keep.tile([P, 2], F32, name="bias_first")
-        bias_rest = keep.tile([P, 2], F32, name="bias_rest")
-
-        def lb(eng):
+        def lb(eng, t0, nt):
             columns = b.rearrange("(t p) o -> p (t o)", p=P)
+            piece = keep.tile([P, nt], F32, name="bias%d" % t0)
             with nc.allow_non_contiguous_dma(reason="one bias value a partition and tile"):
-                eng.dma_start(bias_first[:], columns[:, 0:2])
-                eng.dma_start(bias_rest[:], columns[:, 2:4])
+                eng.dma_start(piece[:], columns[:, t0 : t0 + nt])
+            for t in range(t0, t0 + nt):
+                bias[t] = piece[:, t - t0 : t - t0 + 1]
 
-        segments = keep.tile([P, 32], F32, name="segments", align_bytes=64)
-        turned = keep.tile([P, 32], F32, name="turned", align_bytes=64)
+        seg = {}
+
+        def mb(meng, tag="segments"):
+            seg[0] = keep.tile([P, 32], F32, name="segments", tag=tag, align_bytes=256)
+            meng.memset(seg[0][:], 0.0)
 
         def lbv(eng):
-            nc.vector.memset(segments[:], 0.0)
-            eng.dma_start(segments[0:P:8, :], b.rearrange("(t q j) o -> q t (j o)", t=4, q=4))
+            eng.dma_start(seg[0][0:P:8, :], b.rearrange("(t q j) o -> q t (j o)", t=4, q=4))
 
-        def turn():
-            nc.vector.transpose(turned[:], segments[:])
+        def turn(tag="turned"):
+            turned = keep.tile([P, 32], F32, name="turned", tag=tag, align_bytes=256)
+            nc.vector.transpose(turned[:], seg[0][:])
+            for t in range(4):
+                bias[t] = turned[:, 8 * t : 8 * t + 1]
 
-        words, scales, grouped, accs = {}, {}, {}, {}
-        w_codes = [keep.tile([P, P], U32, name="w_codes%d" % t, align_bytes=64) for t in range(4)]
-        w_scales = [keep.tile([P, P], U8, name="w_scales%d" % t, align_bytes=64) for t in range(4)]
-        act = {}
-        pooled = keep.tile([P, 4, V], F32, name="pooled")
+        words, scales, grouped, accs, act, codes, planes = {}, {}, {}, {}, {}, {}, {}
+        pools = {}
+
+        def pool(t0, nt, tag=None):
+            tile = keep.tile([P, nt * V], F32, name="pooled%d" % t0, tag=tag or "pooled%d" % t0, align_bytes=256)
+            for t in range(t0, t0 + nt):
+                pools[t] = (tile, t0)
 
         def gw(a, n, tag=None):
-            words[a] = keep.tile([P, n], U32, name="words%d" % a, tag=tag or "words%d" % a, align_bytes=64)
+            words[a] = keep.tile([P, n], U32, name="words%d" % a, tag=tag or "words%d" % a, align_bytes=256)
             nc.vector.tensor_copy(words[a][:], word_table[:].bitcast(U32).indirect(offsets[:, a // 16 : (a + n) // 16]))
 
-
-        def gw2(a, n):
-            nc.vector.tensor_copy(words[0][:, a : a + n], word_table[:].bitcast(U32).indirect(offsets[:, a // 16 : (a + n) // 16]))
-
         def gs(a, n, tag=None):
-            scales[a] = keep.tile([P, n], U8, name="scales%d" % a, tag=tag or "scales%d" % a, align_bytes=64)
+            scales[a] = keep.tile([P, n], U8, name="scales%d" % a, tag=tag or "scales%d" % a, align_bytes=256)
             nc.vector.tensor_copy(scales[a][:], scale_table[:].bitcast(U8).indirect(offsets[:, a // 16 : (a + n) // 16]))
 
         def part(table, a, n):
             a0 = max(k for k in table if k <= a)
             return table[a0][:, a - a0 : a - a0 + n]
 
+        def group(t0, nt, tag=None):
+            g = keep.tile([P, nt * P, 4], BF16, name="grouped%d" % t0, tag=tag or "grouped%d" % t0, align_bytes=256)
+            for t in range(t0, t0 + nt):
+                grouped[t] = (g, t0)
+
         def il(t, eng, lo=0, hi=P, tag=None):
             if t not in grouped:
-                grouped[t] = keep.tile([P, P, 4], BF16, name="grouped%d" % t, tag=tag or "grouped%d" % t, align_bytes=64)
-            dst = grouped[t][:, lo:hi, :].rearrange("p (c i) j -> p c j i", i=4)
-            src = raw[t][:, :, lo:hi].rearrange("p j (c i) -> p c j i", i=4)
+                group(t, 1, tag)
+            g, t0 = grouped[t]
+            chunk, c0 = raw[t * P + lo]
+            dst = g[:, (t - t0) * P + lo : (t - t0) * P + hi, :]
+            src = chunk[:, :, t * P + lo - c0 : t * P + hi - c0]
+            dst4 = dst.rearrange("p (c i) j -> p c j i", i=4)
+            src4 = src.rearrange("p j (c i) -> p c j i", i=4)
             if eng == "v":
-                nc.vector.tensor_copy(dst, src)
+                nc.vector.tensor_copy(dst4, src4)
             elif eng == "s":
-                nc.scalar.copy(dst, src)
+                nc.scalar.copy(dst4, src4)
+            elif eng == "g":
+                nc.gpsimd.tensor_scalar(dst4, src4, 1.0, 0.0, MULT, ADD)
+            elif eng == "gc":
+                nc.gpsimd.tensor_scalar(dst, src.rearrange("p j c -> p c j"), 1.0, 0.0, MULT, ADD)
             else:
-                nc.gpsimd.tensor_scalar(dst, src, 1.0, 0.0, mybir.AluOpType.mult, mybir.AluOpType.add)
+                nc.gpsimd.tensor_copy(dst, src.rearrange("p j c -> p c j"))
 
-        def q(t):
-            nc.vector.quantize_mx(out=w_codes[t][:].bitcast(FP8X4), scales=w_scales[t][:], in_=grouped[t][:].rearrange("p c j -> p (c j)"))
+        def q(t, nt=1, tag=None):
+            g, t0 = grouped[t]
+            c = keep.tile([P, nt * P], U32, name="w_codes%d" % t, tag=tag or "w_codes%d" % t, align_bytes=256)
+            s = keep.tile([P, nt * P], U8, name="w_scales%d" % t, align_bytes=256)
+            nc.vector.quantize_mx(out=c[:].bitcast(FP8X4), scales=s[:], in_=g[:, (t - t0) * P : (t - t0 + nt) * P, :].rearrange("p c j -> p (c j)"))
+            for u in range(nt):
+                codes[t + u] = c[:, u * P : (u + 1) * P]
+                planes[t + u] = s[:, u * P : (u + 1) * P]
 
         def mm(t, a, n, bank, col=0):
             if col == 0:
                 accs[bank] = psum.tile([P, 512], F32, name="acc%d_%d" % (t, a), tag="bank%d" % bank)
-            nc.tensor.matmul_mx(out=accs[bank][:, col : col + n], lhsT=w_codes[t][:].bitcast(FP8X4), lhsT_scale=w_scales[t][:],
+            nc.tensor.matmul_mx(out=accs[bank][:, col : col + n], lhsT=codes[t].bitcast(FP8X4), lhsT_scale=planes[t],
                                 rhs=part(words, a, n).bitcast(FP8X4), rhs_scale=part(scales, a, n), start=True, stop=True)
 
-        def place(t, a, n, offset):
-            late = shared.tile([P, n], F32, name="late%d_%d" % (t, a), align_bytes=64, offset=offset)
-            for a0 in range(0, n, 256):
-                act[t, a + a0] = late[:, a0 : a0 + 256]
+        def room(t, a, n, tag=None):
+            tile = keep.tile([P, n], F32, name="act%d_%d" % (t, a), tag=tag or "act%d_%d" % (t, a), align_bytes=256)
+            for c in range(a, a + n, 64):
+                act[t, c] = (tile, a)
 
-        def si(t, a, n, bank, tag=None, col=0):
+        def rooms(u0, nu, tag=None):
+            tile = keep.tile([P, 256 * nu], F32, name="units%d" % u0, tag=tag or "units%d" % u0, align_bytes=256)
+            for c in range(256 * u0, 256 * (u0 + nu), 64):
+                act[c // 512, c % 512] = (tile, 256 * u0 - 512 * (c // 512))
+
+        def rdu(c0, n):
+            tile, a0 = act[c0 // 512, c0 % 512]
+            a = c0 % 512
+            dst, t0 = pools[c0 // 512]
+            nc.vector.tensor_reduce(dst[:, c0 // D - t0 * V : (c0 + n) // D - t0 * V], tile[:, a - a0 : a - a0 + n].rearrange("p (v d) -> p v d", d=D), mybir.AxisListType.X, MAX)
+
+        def si(t, a, n, bank, col=0, tag=None):
             if (t, a) not in act:
-                act[t, a] = keep.tile([P, n], F32, name="act%d_%d" % (t, a), tag=tag or "act%d_%d" % (t, a), align_bytes=64)[:]
-            nc.scalar.activation(act[t, a], accs[bank][:, col : col + n], SILU, bias=bias_first[:, t : t + 1] if t < 2 else bias_rest[:, t - 2 : t - 1])
+                room(t, a, n, tag)
+            tile, a0 = act[t, a]
+            nc.scalar.activation(tile[:, a - a0 : a - a0 + n], accs[bank][:, col : col + n], SILU, bias=bias[t])
 
         def rd(t, a, n):
-            nc.vector.tensor_reduce(pooled[:, t, a // D : (a + n) // D], act[t, a].rearrange("p (v d) -> p v d", d=D), mybir.AxisListType.X, MAX)
-
-        def unit(t, a, n, bank, tag=None):
-            mm(t, a, n, bank)
-            si(t, a, n, bank, tag)
-            rd(t, a, n)
-
-        def unit2(t, bank, tag=None):
-            mm(t, 0, 256, bank)
-            mm(t, 256, 256, bank, 256)
-            si(t, 0, 512, bank, tag)
-            rd(t, 0, 512)
+            tile, a0 = act[t, a]
+            dst, t0 = pools[t]
+            nc.vector.tensor_reduce(dst[:, (t - t0) * V + a // D : (t - t0) * V + (a + n) // D], tile[:, a - a0 : a - a0 + n].rearrange("p (v d) -> p v d", d=D), mybir.AxisListType.X, MAX)
 
         def st(t, nt=1, eng=nc.sync):
-            eng.dma_start(out.rearrange("(t p) v -> p t v", p=P)[:, t : t + nt, :], pooled[:, t : t + nt, :])
+            eng.dma_start(out.rearrange("(t p) v -> p t v", p=P)[:, t : t + nt, :], pools[t][0][:, (t - pools[t][1]) * V : (t - pools[t][1] + nt) * V].rearrange("p (t v) -> p t v", v=V))
 
         def probe(ap, k):
             pr = keep.tile([P, 1], ap.dtype, name="probe%d" % k)
             nc.gpsimd.tensor_copy(pr[:], ap)
+
+        def clock(eng, ap, k):
+            pr = keep.tile([P, 1], ap.dtype, name="clock%d" % k)
+            if eng is nc.scalar:
+                eng.copy(pr[:], ap)
+            else:
+                eng.tensor_copy(pr[:], ap)
 
         sy, sc, gp, ve = nc.sync, nc.scalar, nc.gpsimd, nc.vector
         ms(ve)
@@ -167,10 +194,11 @@ def tile_picked_pool_lin_silu_sub_p_kernel(tc, x_words, x_scales, w, b, offs, ou
         ls(sy,1)
         lw(sy,0,128)
         lw(sy,128,128)
-        lw(sy,256,128)
-        lw(sy,384,128)
-        lb(sy)
+        lw(sy,256,256)
+        lb(sy,0,2)
+        lb(sy,2,2)
 
+        pool(0,4)
         gw(0,512)
         gs(0,256)
         il(0,"s")
@@ -183,14 +211,14 @@ def tile_picked_pool_lin_silu_sub_p_kernel(tc, x_words, x_scales, w, b, offs, ou
         gs(256,256,"w_raw128")
         mm(0,256,256,2)
         mm(1,256,256,3)
-        il(3,"s",0,64)
-        il(3,"g",64,128)
+        il(3,"gc")
         q(2)
         q(3)
         mm(2,0,256,4)
         mm(2,256,256,5)
         mm(3,0,256,6)
         mm(3,256,256,7)
+
         si(0,0,256,0)
         rd(0,0,256)
         si(1,0,256,1)
@@ -207,7 +235,7 @@ def tile_picked_pool_lin_silu_sub_p_kernel(tc, x_words, x_scales, w, b, offs, ou
         st(2)
         si(3,0,256,6)
         si(3,256,128,7)
-        si(3,384,128,7,None,128)
+        si(3,384,128,7,128)
         rd(3,0,256)
         rd(3,256,128)
         rd(3,384,128)

@@ -25,9 +25,16 @@ def tile_picked_pool_lin_silu_sub_p_kernel(tc, x_words, x_scales, w, b, offs, ou
         keep = ctx.enter_context(tc.tile_pool(name="keep", bufs=1))
         psum = ctx.enter_context(tc.psum_pool(name="psum", bufs=1))
 
+        held = ctx.enter_context(tc.tile_pool(name="held", bufs=1))
+
+        def place(shape, dtype, name, tag):
+            if isinstance(tag, int):
+                return held.tile(shape, dtype, name=name, tag=name, offset=tag, align_bytes=256)
+            return keep.tile(shape, dtype, name=name, tag=tag, align_bytes=256)
+
         offsets = keep.tile([P, S // 16], U16, name="offsets")
         word_table = keep.tile([P, T], I32, name="word_table", align_bytes=256)
-        scale_table = keep.tile([P, T // 4], I32, name="scale_table", tag="scale_table", align_bytes=256)
+        scale_table = place([P, T // 4], I32, "scale_table", "scale_table")
         scale_rows = x_scales[0].bitcast(I32)
         w_rows = w.rearrange("(p j) n -> p j n", j=4)
         raw, bias = {}, {}
@@ -50,11 +57,21 @@ def tile_picked_pool_lin_silu_sub_p_kernel(tc, x_words, x_scales, w, b, offs, ou
         def ls(eng, q):
             eng.dma_start(scale_table[32 * q : 32 * q + 4, :], scale_rows[4 * q : 4 * q + 4, :])
 
+        staged = {}
+
+        def lst(eng, q):
+            if 0 not in staged:
+                staged[0] = place([P, T // 4], I32, "scale_staged", "scale_staged")
+            eng.dma_start(staged[0][32 * q : 32 * q + 4, :], scale_rows[4 * q : 4 * q + 4, :])
+
+        def cs(q):
+            nc.vector.tensor_copy(scale_table[32 * q : 32 * q + 4, :], staged[0][32 * q : 32 * q + 4, :])
+
         def lsr(eng, q):
             eng.dma_start(scale_table[32 * q : 32 * q + 32, :], scale_rows[4 * q : 4 * q + 4, :].partition_broadcast(8))
 
         def lw(eng, c0, width, tag=None):
-            chunk = keep.tile([P, 4, width], F32, name="w_raw%d" % c0, tag=tag or "w_raw%d" % c0, align_bytes=256)
+            chunk = place([P, 4, width], F32, "w_raw%d" % c0, tag or "w_raw%d" % c0)
             eng.dma_start(chunk[:], w_rows[:, :, c0 : c0 + width])
             for c in range(c0, c0 + width, 32):
                 raw[c] = (chunk, c0)
@@ -70,14 +87,14 @@ def tile_picked_pool_lin_silu_sub_p_kernel(tc, x_words, x_scales, w, b, offs, ou
         seg = {}
 
         def mb(meng, tag="segments"):
-            seg[0] = keep.tile([P, 32], F32, name="segments", tag=tag, align_bytes=256)
+            seg[0] = place([P, 32], F32, "segments", tag)
             meng.memset(seg[0][:], 0.0)
 
         def lbv(eng):
             eng.dma_start(seg[0][0:P:8, :], b.rearrange("(t q j) o -> q t (j o)", t=4, q=4))
 
         def turn(tag="turned"):
-            turned = keep.tile([P, 32], F32, name="turned", tag=tag, align_bytes=256)
+            turned = place([P, 32], F32, "turned", tag)
             nc.vector.transpose(turned[:], seg[0][:])
             for t in range(4):
                 bias[t] = turned[:, 8 * t : 8 * t + 1]
@@ -86,16 +103,21 @@ def tile_picked_pool_lin_silu_sub_p_kernel(tc, x_words, x_scales, w, b, offs, ou
         pools = {}
 
         def pool(t0, nt, tag=None):
-            tile = keep.tile([P, nt * V], F32, name="pooled%d" % t0, tag=tag or "pooled%d" % t0, align_bytes=256)
+            tile = place([P, nt * V], F32, "pooled%d" % t0, tag or "pooled%d" % t0)
             for t in range(t0, t0 + nt):
                 pools[t] = (tile, t0)
 
         def gw(a, n, tag=None):
-            words[a] = keep.tile([P, n], U32, name="words%d" % a, tag=tag or "words%d" % a, align_bytes=256)
+            words[a] = place([P, n], U32, "words%d" % a, tag or "words%d" % a)
             nc.vector.tensor_copy(words[a][:], word_table[:].bitcast(U32).indirect(offsets[:, a // 16 : (a + n) // 16]))
 
+        def gwi(a, n, tag="words0"):
+            if 0 not in words:
+                words[0] = place([P, S], U32, "words0", tag)
+            nc.vector.tensor_copy(words[0][:, a : a + n], word_table[:].bitcast(U32).indirect(offsets[:, a // 16 : (a + n) // 16]))
+
         def gs(a, n, tag=None):
-            scales[a] = keep.tile([P, n], U8, name="scales%d" % a, tag=tag or "scales%d" % a, align_bytes=256)
+            scales[a] = place([P, n], U8, "scales%d" % a, tag or "scales%d" % a)
             nc.vector.tensor_copy(scales[a][:], scale_table[:].bitcast(U8).indirect(offsets[:, a // 16 : (a + n) // 16]))
 
         def part(table, a, n):
@@ -103,9 +125,14 @@ def tile_picked_pool_lin_silu_sub_p_kernel(tc, x_words, x_scales, w, b, offs, ou
             return table[a0][:, a - a0 : a - a0 + n]
 
         def group(t0, nt, tag=None):
-            g = keep.tile([P, nt * P, 4], BF16, name="grouped%d" % t0, tag=tag or "grouped%d" % t0, align_bytes=256)
+            g = place([P, nt * P, 4], BF16, "grouped%d" % t0, tag or "grouped%d" % t0)
             for t in range(t0, t0 + nt):
                 grouped[t] = (g, t0)
+
+        def groupx(ts, tag):
+            g = place([P, len(ts) * P, 4], BF16, "groupedx%d" % ts[0], tag)
+            for u, t in enumerate(ts):
+                grouped[t] = (g, t - u)
 
         def il(t, eng, lo=0, hi=P, tag=None):
             if t not in grouped:
@@ -129,12 +156,32 @@ def tile_picked_pool_lin_silu_sub_p_kernel(tc, x_words, x_scales, w, b, offs, ou
 
         def q(t, nt=1, tag=None):
             g, t0 = grouped[t]
-            c = keep.tile([P, nt * P], U32, name="w_codes%d" % t, tag=tag or "w_codes%d" % t, align_bytes=256)
+            c = place([P, nt * P], U32, "w_codes%d" % t, tag or "w_codes%d" % t)
             s = keep.tile([P, nt * P], U8, name="w_scales%d" % t, align_bytes=256)
             nc.vector.quantize_mx(out=c[:].bitcast(FP8X4), scales=s[:], in_=g[:, (t - t0) * P : (t - t0 + nt) * P, :].rearrange("p c j -> p (c j)"))
             for u in range(nt):
                 codes[t + u] = c[:, u * P : (u + 1) * P]
                 planes[t + u] = s[:, u * P : (u + 1) * P]
+
+        shared = {}
+
+        def qs(t, key, nt, slot, tag=None):
+            g, t0 = grouped[t]
+            if key not in shared:
+                shared[key] = place([P, nt * P], U32, "w_codes_" + key, tag or "w_codes_" + key)
+            c = shared[key][:, slot * P : (slot + 1) * P]
+            s = keep.tile([P, P], U8, name="w_scales%d" % t, align_bytes=256)
+            nc.vector.quantize_mx(out=c.bitcast(FP8X4), scales=s[:], in_=g[:, (t - t0) * P : (t - t0 + 1) * P, :].rearrange("p c j -> p (c j)"))
+            codes[t] = c
+            planes[t] = s[:]
+
+        def roomx(key, units, tag=None):
+            tile = place([P, sum(n for t, a, n in units)], F32, "act_" + key, tag or "act_" + key)
+            at = 0
+            for t, a, n in units:
+                for c in range(a, a + n, 64):
+                    act[t, c] = (tile, a - at)
+                at = at + n
 
         def mm(t, a, n, bank, col=0):
             if col == 0:
@@ -143,12 +190,12 @@ def tile_picked_pool_lin_silu_sub_p_kernel(tc, x_words, x_scales, w, b, offs, ou
                                 rhs=part(words, a, n).bitcast(FP8X4), rhs_scale=part(scales, a, n), start=True, stop=True)
 
         def room(t, a, n, tag=None):
-            tile = keep.tile([P, n], F32, name="act%d_%d" % (t, a), tag=tag or "act%d_%d" % (t, a), align_bytes=256)
+            tile = place([P, n], F32, "act%d_%d" % (t, a), tag or "act%d_%d" % (t, a))
             for c in range(a, a + n, 64):
                 act[t, c] = (tile, a)
 
         def rooms(u0, nu, tag=None):
-            tile = keep.tile([P, 256 * nu], F32, name="units%d" % u0, tag=tag or "units%d" % u0, align_bytes=256)
+            tile = place([P, 256 * nu], F32, "units%d" % u0, tag or "units%d" % u0)
             for c in range(256 * u0, 256 * (u0 + nu), 64):
                 act[c // 512, c % 512] = (tile, 256 * u0 - 512 * (c // 512))
 
@@ -168,6 +215,11 @@ def tile_picked_pool_lin_silu_sub_p_kernel(tc, x_words, x_scales, w, b, offs, ou
             tile, a0 = act[t, a]
             dst, t0 = pools[t]
             nc.vector.tensor_reduce(dst[:, (t - t0) * V + a // D : (t - t0) * V + (a + n) // D], tile[:, a - a0 : a - a0 + n].rearrange("p (v d) -> p v d", d=D), mybir.AxisListType.X, MAX)
+
+        def rdx(t, nt, a, n):
+            tile, a0 = act[t, a]
+            dst, t0 = pools[t]
+            nc.vector.tensor_reduce(dst[:].rearrange("p (t v) -> p t v", v=V)[:, t - t0 : t - t0 + nt, a // D : (a + n) // D], tile[:, a - a0 : a - a0 + nt * n].rearrange("p (t v d) -> p t v d", t=nt, d=D), mybir.AxisListType.X, MAX)
 
         def st(t, nt=1, eng=nc.sync):
             eng.dma_start(out.rearrange("(t p) v -> p t v", p=P)[:, t : t + nt, :], pools[t][0][:, (t - pools[t][1]) * V : (t - pools[t][1] + nt) * V].rearrange("p (t v) -> p t v", v=V))
@@ -203,7 +255,6 @@ def tile_picked_pool_lin_silu_sub_p_kernel(tc, x_words, x_scales, w, b, offs, ou
         gs(0,256)
         il(0,"s")
         il(1,"s")
-        il(2,"s")
         q(0)
         mm(0,0,256,0)
         q(1)
@@ -211,7 +262,9 @@ def tile_picked_pool_lin_silu_sub_p_kernel(tc, x_words, x_scales, w, b, offs, ou
         gs(256,256,"w_raw128")
         mm(0,256,256,2)
         mm(1,256,256,3)
-        il(3,"gc")
+        il(3,"s",0,96)
+        il(2,"v")
+        il(3,"v",96,128)
         q(2)
         q(3)
         mm(2,0,256,4)

@@ -120,6 +120,11 @@ def tile_picked_pool_lin_silu_sub_p_kernel(tc, x_words, x_scales, w, b, offs, ou
             scales[a] = place([P, n], U8, "scales%d" % a, tag or "scales%d" % a)
             nc.vector.tensor_copy(scales[a][:], scale_table[:].bitcast(U8).indirect(offsets[:, a // 16 : (a + n) // 16]))
 
+        def gsi(base, total, a, n, tag):
+            if base not in scales:
+                scales[base] = place([P, total], U8, "scales%d" % base, tag)
+            nc.vector.tensor_copy(scales[base][:, a - base : a - base + n], scale_table[:].bitcast(U8).indirect(offsets[:, a // 16 : (a + n) // 16]))
+
         def part(table, a, n):
             a0 = max(k for k in table if k <= a)
             return table[a0][:, a - a0 : a - a0 + n]
@@ -249,7 +254,6 @@ def tile_picked_pool_lin_silu_sub_p_kernel(tc, x_words, x_scales, w, b, offs, ou
         lw(sy,256,256)
         lb(sy,0,2)
         lb(sy,2,2)
-
         pool(0,4)
         gw(0,512)
         gs(0,256)
@@ -259,36 +263,43 @@ def tile_picked_pool_lin_silu_sub_p_kernel(tc, x_words, x_scales, w, b, offs, ou
         mm(0,0,256,0)
         q(1)
         mm(1,0,256,1)
-        gs(256,256,"w_raw128")
-        mm(0,256,256,2)
-        mm(1,256,256,3)
-        il(3,"s",0,96)
-        il(2,"v")
-        il(3,"v",96,128)
+        gsi(256,256,256,128,"w_raw128")
+        mm(0,256,128,2)
+        mm(1,256,128,3)
+        gsi(256,256,384,128,"w_raw128")
+        mm(0,384,128,4)
+        mm(1,384,128,5)
+        il(2,"s",0,96)
+        il(2,"v",96,128)
+        il(3,"gc")
         q(2)
         q(3)
-        mm(2,0,256,4)
-        mm(2,256,256,5)
-        mm(3,0,256,6)
-        mm(3,256,256,7)
-
+        mm(2,0,256,6)
+        mm(2,256,256,7)
         si(0,0,256,0)
         rd(0,0,256)
         si(1,0,256,1)
         rd(1,0,256)
-        si(0,256,256,2)
+        mm(3,0,256,0)
+        mm(3,256,128,1)
+        room(0,256,256)
+        room(1,256,256)
+        si(0,256,128,2)
+        mm(3,384,128,2)
+        si(1,256,128,3)
+        si(0,384,128,4)
         rd(0,256,256)
-        si(1,256,256,3)
+        si(1,384,128,5)
         rd(1,256,256)
         st(0,2)
-        si(2,0,256,4)
-        si(2,256,256,5)
+        si(2,0,256,6)
+        si(2,256,256,7)
         rd(2,0,256)
         rd(2,256,256)
         st(2)
-        si(3,0,256,6)
-        si(3,256,128,7)
-        si(3,384,128,7,128)
+        si(3,0,256,0)
+        si(3,256,128,1)
+        si(3,384,128,2)
         rd(3,0,256)
         rd(3,256,128)
         rd(3,384,128)

@@ -269,8 +269,7 @@ def tile_picked_pool_lin_silu_sub_p_kernel(tc, x_words, x_scales, w, b, offs, ou
         gsi(256,256,384,128,"w_raw128")
         mm(0,384,128,4)
         mm(1,384,128,5)
-        il(2,"s",0,96)
-        il(2,"v",96,128)
+        il(2,"s")
         il(3,"gc")
         q(2)
         q(3)

@@ -16,7 +16,15 @@ SILU = mybir.ActivationFunctionType.Silu
 MAX = mybir.AluOpType.max
 MULT = mybir.AluOpType.mult
 ADD = mybir.AluOpType.add
+
 P = 128
+PACK = 4
+QUADRANT = 32
+PER_COLUMN = 16
+BANK = 512
+ALIGN = 256
+HALF = S // 2
+QUARTER = S // 4
 
 
 def tile_picked_pool_lin_silu_sub_p_kernel(tc, x_words, x_scales, w, b, offs, out):
@@ -25,281 +33,158 @@ def tile_picked_pool_lin_silu_sub_p_kernel(tc, x_words, x_scales, w, b, offs, ou
         keep = ctx.enter_context(tc.tile_pool(name="keep", bufs=1))
         psum = ctx.enter_context(tc.psum_pool(name="psum", bufs=1))
 
-        held = ctx.enter_context(tc.tile_pool(name="held", bufs=1))
+        def aligned(shape, dtype, name, tag=None):
+            return keep.tile(shape, dtype, name=name, tag=tag or name, align_bytes=ALIGN)
 
-        def place(shape, dtype, name, tag):
-            if isinstance(tag, int):
-                return held.tile(shape, dtype, name=name, tag=name, offset=tag, align_bytes=256)
-            return keep.tile(shape, dtype, name=name, tag=tag, align_bytes=256)
+        offsets = keep.tile([P, S // PER_COLUMN], U16, name="offsets")
+        word_table = aligned([P, T], I32, "word_table")
+        scale_table = aligned([P, T // 4], I32, "scale_table")
 
-        offsets = keep.tile([P, S // 16], U16, name="offsets")
-        word_table = keep.tile([P, T], I32, name="word_table", align_bytes=256)
-        scale_table = place([P, T // 4], I32, "scale_table", "scale_table")
-        scale_rows = x_scales[0].bitcast(I32)
-        w_rows = w.rearrange("(p j) n -> p j n", j=4)
-        raw, bias = {}, {}
+        def load_scale_rows(queue, quadrant):
+            rows = x_scales[0].bitcast(I32)[PACK * quadrant : PACK * (quadrant + 1), :]
+            queue.dma_start(scale_table[QUADRANT * quadrant : QUADRANT * quadrant + PACK, :], rows)
 
-        def ms(eng, lo=0, hi=T // 4):
-            eng.memset(scale_table[:, lo:hi], 0)
+        nc.vector.memset(scale_table[:], 0)
+        nc.sync.dma_start(offsets[:], offs)
+        nc.sync.dma_start(word_table[:], x_words[0].rearrange("p c r -> p (c r)").bitcast(I32))
+        load_scale_rows(nc.scalar, 2)
+        load_scale_rows(nc.scalar, 3)
 
-        def warm(eng):
-            warm_in = keep.tile([P, 8], F32, name="warm_in")
-            warm_out = keep.tile([P, 8], F32, name="warm_out")
-            eng.memset(warm_in[:], 0.0)
-            nc.scalar.activation(warm_out[:], warm_in[:], SILU)
+        warm_in = keep.tile([P, 8], F32, name="warm_in")
+        warm_out = keep.tile([P, 8], F32, name="warm_out")
+        nc.vector.memset(warm_in[:], 0.0)
+        nc.scalar.activation(warm_out[:], warm_in[:], SILU)
 
-        def lx(eng):
-            eng.dma_start(word_table[:], x_words[0].rearrange("p c r -> p (c r)").bitcast(I32))
+        load_scale_rows(nc.sync, 0)
+        load_scale_rows(nc.sync, 1)
 
-        def lo():
-            nc.sync.dma_start(offsets[:], offs)
+        w_rows = w.rearrange("(p j) n -> p j n", j=PACK)
+        w_raw = []
+        for first, count in ((0, 1), (1, 1), (2, 2)):
+            chunk = aligned([P, PACK, count * P], F32, "w_raw%d" % (first * P))
+            nc.sync.dma_start(chunk[:], w_rows[:, :, first * P : (first + count) * P])
+            w_raw.extend(chunk[:, :, u * P : (u + 1) * P] for u in range(count))
 
-        def ls(eng, q):
-            eng.dma_start(scale_table[32 * q : 32 * q + 4, :], scale_rows[4 * q : 4 * q + 4, :])
+        bias = []
+        for first in (0, 2):
+            pair = keep.tile([P, 2], F32, name="bias%d" % first)
+            with nc.allow_non_contiguous_dma(reason="one bias value a partition and channel tile"):
+                nc.sync.dma_start(pair[:], b.rearrange("(t p) o -> p (t o)", p=P)[:, first : first + 2])
+            bias.extend(pair[:, u : u + 1] for u in range(2))
 
-        staged = {}
+        pooled = aligned([P, 4 * V], F32, "pooled")
 
-        def lst(eng, q):
-            if 0 not in staged:
-                staged[0] = place([P, T // 4], I32, "scale_staged", "scale_staged")
-            eng.dma_start(staged[0][32 * q : 32 * q + 4, :], scale_rows[4 * q : 4 * q + 4, :])
+        def gather(dst, table, first, count):
+            entries = offsets[:, first // PER_COLUMN : (first + count) // PER_COLUMN]
+            nc.vector.tensor_copy(dst, table.indirect(entries))
 
-        def cs(q):
-            nc.vector.tensor_copy(scale_table[32 * q : 32 * q + 4, :], staged[0][32 * q : 32 * q + 4, :])
+        grouped, w_codes, w_scales, sums, acts = {}, {}, {}, {}, {}
 
-        def lsr(eng, q):
-            eng.dma_start(scale_table[32 * q : 32 * q + 32, :], scale_rows[4 * q : 4 * q + 4, :].partition_broadcast(8))
+        def interleave_on_scalar(t):
+            grouped[t] = aligned([P, P, PACK], BF16, "grouped%d" % t)
+            nc.scalar.copy(
+                grouped[t][:].rearrange("p (c i) j -> p c j i", i=4),
+                w_raw[t].rearrange("p j (c i) -> p c j i", i=4),
+            )
 
-        def lw(eng, c0, width, tag=None):
-            chunk = place([P, 4, width], F32, "w_raw%d" % c0, tag or "w_raw%d" % c0)
-            eng.dma_start(chunk[:], w_rows[:, :, c0 : c0 + width])
-            for c in range(c0, c0 + width, 32):
-                raw[c] = (chunk, c0)
+        def interleave_on_gpsimd(t):
+            grouped[t] = aligned([P, P, PACK], BF16, "grouped%d" % t)
+            nc.gpsimd.tensor_scalar(grouped[t][:], w_raw[t].rearrange("p j c -> p c j"), 1.0, 0.0, MULT, ADD)
 
-        def lb(eng, t0, nt):
-            columns = b.rearrange("(t p) o -> p (t o)", p=P)
-            piece = keep.tile([P, nt], F32, name="bias%d" % t0)
-            with nc.allow_non_contiguous_dma(reason="one bias value a partition and tile"):
-                eng.dma_start(piece[:], columns[:, t0 : t0 + nt])
-            for t in range(t0, t0 + nt):
-                bias[t] = piece[:, t - t0 : t - t0 + 1]
+        def quantize(t):
+            w_codes[t] = aligned([P, P], U32, "w_codes%d" % t)
+            w_scales[t] = aligned([P, P], U8, "w_scales%d" % t)
+            nc.vector.quantize_mx(
+                out=w_codes[t][:].bitcast(FP8X4),
+                scales=w_scales[t][:],
+                in_=grouped[t][:].rearrange("p c j -> p (c j)"),
+            )
 
-        seg = {}
+        def multiply(t, first, count, bank):
+            sums[t, first] = psum.tile([P, BANK], F32, name="sums%d_%d" % (t, first), tag="bank%d" % bank)
+            nc.tensor.matmul_mx(
+                out=sums[t, first][:, 0:count],
+                lhsT=w_codes[t][:].bitcast(FP8X4),
+                lhsT_scale=w_scales[t][:],
+                rhs=words[:, first : first + count].bitcast(FP8X4),
+                rhs_scale=scales[first // HALF][:, first % HALF : first % HALF + count],
+                start=True,
+                stop=True,
+            )
 
-        def mb(meng, tag="segments"):
-            seg[0] = place([P, 32], F32, "segments", tag)
-            meng.memset(seg[0][:], 0.0)
+        def make_room(t, first, count):
+            tile = aligned([P, count], F32, "act%d_%d" % (t, first))
+            for start in range(first, first + count, QUARTER):
+                acts[t, start] = tile[:, start - first : count]
 
-        def lbv(eng):
-            eng.dma_start(seg[0][0:P:8, :], b.rearrange("(t q j) o -> q t (j o)", t=4, q=4))
+        def activate(t, first, count):
+            if (t, first) not in acts:
+                make_room(t, first, count)
+            nc.scalar.activation(acts[t, first][:, 0:count], sums[t, first][:, 0:count], SILU, bias=bias[t])
 
-        def turn(tag="turned"):
-            turned = place([P, 32], F32, "turned", tag)
-            nc.vector.transpose(turned[:], seg[0][:])
-            for t in range(4):
-                bias[t] = turned[:, 8 * t : 8 * t + 1]
+        def take_maxima(t, first, count):
+            nc.vector.tensor_reduce(
+                pooled[:, t * V + first // D : t * V + (first + count) // D],
+                acts[t, first][:, 0:count].rearrange("p (v d) -> p v d", d=D),
+                mybir.AxisListType.X,
+                MAX,
+            )
 
-        words, scales, grouped, accs, act, codes, planes = {}, {}, {}, {}, {}, {}, {}
-        pools = {}
+        def store(t, tiles):
+            nc.sync.dma_start(
+                out.rearrange("(t p) v -> p t v", p=P)[:, t : t + tiles, :],
+                pooled[:, t * V : (t + tiles) * V].rearrange("p (t v) -> p t v", v=V),
+            )
 
-        def pool(t0, nt, tag=None):
-            tile = place([P, nt * V], F32, "pooled%d" % t0, tag or "pooled%d" % t0)
-            for t in range(t0, t0 + nt):
-                pools[t] = (tile, t0)
+        scale_bytes = scale_table[:].bitcast(U8)
+        words = aligned([P, S], U32, "words")
+        gather(words[:], word_table[:].bitcast(U32), 0, S)
+        scales = [aligned([P, HALF], U8, "scales0")]
+        gather(scales[0][:], scale_bytes, 0, HALF)
+        for t in (0, 1):
+            interleave_on_scalar(t)
+        for t in (0, 1):
+            quantize(t)
+            multiply(t, 0, HALF, bank=t)
 
-        def gw(a, n, tag=None):
-            words[a] = place([P, n], U32, "words%d" % a, tag or "words%d" % a)
-            nc.vector.tensor_copy(words[a][:], word_table[:].bitcast(U32).indirect(offsets[:, a // 16 : (a + n) // 16]))
+        scales.append(aligned([P, HALF], U8, "scales1", tag="w_raw%d" % P))
+        for quarter in (0, 1):
+            first = HALF + quarter * QUARTER
+            gather(scales[1][:, quarter * QUARTER : (quarter + 1) * QUARTER], scale_bytes, first, QUARTER)
+            for t in (0, 1):
+                multiply(t, first, QUARTER, bank=2 + 2 * quarter + t)
 
-        def gwi(a, n, tag="words0"):
-            if 0 not in words:
-                words[0] = place([P, S], U32, "words0", tag)
-            nc.vector.tensor_copy(words[0][:, a : a + n], word_table[:].bitcast(U32).indirect(offsets[:, a // 16 : (a + n) // 16]))
+        interleave_on_scalar(2)
+        interleave_on_gpsimd(3)
+        quantize(2)
+        quantize(3)
+        for half in (0, 1):
+            multiply(2, half * HALF, HALF, bank=6 + half)
 
-        def gs(a, n, tag=None):
-            scales[a] = place([P, n], U8, "scales%d" % a, tag or "scales%d" % a)
-            nc.vector.tensor_copy(scales[a][:], scale_table[:].bitcast(U8).indirect(offsets[:, a // 16 : (a + n) // 16]))
+        for t in (0, 1):
+            activate(t, 0, HALF)
+            take_maxima(t, 0, HALF)
+        multiply(3, 0, HALF, bank=0)
+        multiply(3, HALF, QUARTER, bank=1)
+        for t in (0, 1):
+            make_room(t, HALF, HALF)
+        activate(0, HALF, QUARTER)
+        multiply(3, HALF + QUARTER, QUARTER, bank=2)
+        activate(1, HALF, QUARTER)
+        for t in (0, 1):
+            activate(t, HALF + QUARTER, QUARTER)
+            take_maxima(t, HALF, HALF)
+        store(0, 2)
 
-        def gsi(base, total, a, n, tag):
-            if base not in scales:
-                scales[base] = place([P, total], U8, "scales%d" % base, tag)
-            nc.vector.tensor_copy(scales[base][:, a - base : a - base + n], scale_table[:].bitcast(U8).indirect(offsets[:, a // 16 : (a + n) // 16]))
+        for half in (0, 1):
+            activate(2, half * HALF, HALF)
+        for half in (0, 1):
+            take_maxima(2, half * HALF, HALF)
+        store(2, 1)
 
-        def part(table, a, n):
-            a0 = max(k for k in table if k <= a)
-            return table[a0][:, a - a0 : a - a0 + n]
-
-        def group(t0, nt, tag=None):
-            g = place([P, nt * P, 4], BF16, "grouped%d" % t0, tag or "grouped%d" % t0)
-            for t in range(t0, t0 + nt):
-                grouped[t] = (g, t0)
-
-        def groupx(ts, tag):
-            g = place([P, len(ts) * P, 4], BF16, "groupedx%d" % ts[0], tag)
-            for u, t in enumerate(ts):
-                grouped[t] = (g, t - u)
-
-        def il(t, eng, lo=0, hi=P, tag=None):
-            if t not in grouped:
-                group(t, 1, tag)
-            g, t0 = grouped[t]
-            chunk, c0 = raw[t * P + lo]
-            dst = g[:, (t - t0) * P + lo : (t - t0) * P + hi, :]
-            src = chunk[:, :, t * P + lo - c0 : t * P + hi - c0]
-            dst4 = dst.rearrange("p (c i) j -> p c j i", i=4)
-            src4 = src.rearrange("p j (c i) -> p c j i", i=4)
-            if eng == "v":
-                nc.vector.tensor_copy(dst4, src4)
-            elif eng == "s":
-                nc.scalar.copy(dst4, src4)
-            elif eng == "g":
-                nc.gpsimd.tensor_scalar(dst4, src4, 1.0, 0.0, MULT, ADD)
-            elif eng == "gc":
-                nc.gpsimd.tensor_scalar(dst, src.rearrange("p j c -> p c j"), 1.0, 0.0, MULT, ADD)
-            else:
-                nc.gpsimd.tensor_copy(dst, src.rearrange("p j c -> p c j"))
-
-        def q(t, nt=1, tag=None):
-            g, t0 = grouped[t]
-            c = place([P, nt * P], U32, "w_codes%d" % t, tag or "w_codes%d" % t)
-            s = keep.tile([P, nt * P], U8, name="w_scales%d" % t, align_bytes=256)
-            nc.vector.quantize_mx(out=c[:].bitcast(FP8X4), scales=s[:], in_=g[:, (t - t0) * P : (t - t0 + nt) * P, :].rearrange("p c j -> p (c j)"))
-            for u in range(nt):
-                codes[t + u] = c[:, u * P : (u + 1) * P]
-                planes[t + u] = s[:, u * P : (u + 1) * P]
-
-        shared = {}
-
-        def qs(t, key, nt, slot, tag=None):
-            g, t0 = grouped[t]
-            if key not in shared:
-                shared[key] = place([P, nt * P], U32, "w_codes_" + key, tag or "w_codes_" + key)
-            c = shared[key][:, slot * P : (slot + 1) * P]
-            s = keep.tile([P, P], U8, name="w_scales%d" % t, align_bytes=256)
-            nc.vector.quantize_mx(out=c.bitcast(FP8X4), scales=s[:], in_=g[:, (t - t0) * P : (t - t0 + 1) * P, :].rearrange("p c j -> p (c j)"))
-            codes[t] = c
-            planes[t] = s[:]
-
-        def roomx(key, units, tag=None):
-            tile = place([P, sum(n for t, a, n in units)], F32, "act_" + key, tag or "act_" + key)
-            at = 0
-            for t, a, n in units:
-                for c in range(a, a + n, 64):
-                    act[t, c] = (tile, a - at)
-                at = at + n
-
-        def mm(t, a, n, bank, col=0):
-            if col == 0:
-                accs[bank] = psum.tile([P, 512], F32, name="acc%d_%d" % (t, a), tag="bank%d" % bank)
-            nc.tensor.matmul_mx(out=accs[bank][:, col : col + n], lhsT=codes[t].bitcast(FP8X4), lhsT_scale=planes[t],
-                                rhs=part(words, a, n).bitcast(FP8X4), rhs_scale=part(scales, a, n), start=True, stop=True)
-
-        def room(t, a, n, tag=None):
-            tile = place([P, n], F32, "act%d_%d" % (t, a), tag or "act%d_%d" % (t, a))
-            for c in range(a, a + n, 64):
-                act[t, c] = (tile, a)
-
-        def rooms(u0, nu, tag=None):
-            tile = place([P, 256 * nu], F32, "units%d" % u0, tag or "units%d" % u0)
-            for c in range(256 * u0, 256 * (u0 + nu), 64):
-                act[c // 512, c % 512] = (tile, 256 * u0 - 512 * (c // 512))
-
-        def rdu(c0, n):
-            tile, a0 = act[c0 // 512, c0 % 512]
-            a = c0 % 512
-            dst, t0 = pools[c0 // 512]
-            nc.vector.tensor_reduce(dst[:, c0 // D - t0 * V : (c0 + n) // D - t0 * V], tile[:, a - a0 : a - a0 + n].rearrange("p (v d) -> p v d", d=D), mybir.AxisListType.X, MAX)
-
-        def si(t, a, n, bank, col=0, tag=None):
-            if (t, a) not in act:
-                room(t, a, n, tag)
-            tile, a0 = act[t, a]
-            nc.scalar.activation(tile[:, a - a0 : a - a0 + n], accs[bank][:, col : col + n], SILU, bias=bias[t])
-
-        def rd(t, a, n):
-            tile, a0 = act[t, a]
-            dst, t0 = pools[t]
-            nc.vector.tensor_reduce(dst[:, (t - t0) * V + a // D : (t - t0) * V + (a + n) // D], tile[:, a - a0 : a - a0 + n].rearrange("p (v d) -> p v d", d=D), mybir.AxisListType.X, MAX)
-
-        def rdx(t, nt, a, n):
-            tile, a0 = act[t, a]
-            dst, t0 = pools[t]
-            nc.vector.tensor_reduce(dst[:].rearrange("p (t v) -> p t v", v=V)[:, t - t0 : t - t0 + nt, a // D : (a + n) // D], tile[:, a - a0 : a - a0 + nt * n].rearrange("p (t v d) -> p t v d", t=nt, d=D), mybir.AxisListType.X, MAX)
-
-        def st(t, nt=1, eng=nc.sync):
-            eng.dma_start(out.rearrange("(t p) v -> p t v", p=P)[:, t : t + nt, :], pools[t][0][:, (t - pools[t][1]) * V : (t - pools[t][1] + nt) * V].rearrange("p (t v) -> p t v", v=V))
-
-        def probe(ap, k):
-            pr = keep.tile([P, 1], ap.dtype, name="probe%d" % k)
-            nc.gpsimd.tensor_copy(pr[:], ap)
-
-        def clock(eng, ap, k):
-            pr = keep.tile([P, 1], ap.dtype, name="clock%d" % k)
-            if eng is nc.scalar:
-                eng.copy(pr[:], ap)
-            else:
-                eng.tensor_copy(pr[:], ap)
-
-        sy, sc, gp, ve = nc.sync, nc.scalar, nc.gpsimd, nc.vector
-        ms(ve)
-        lo()
-        lx(sy)
-        ls(sc,2)
-        ls(sc,3)
-        warm(ve)
-        ls(sy,0)
-        ls(sy,1)
-        lw(sy,0,128)
-        lw(sy,128,128)
-        lw(sy,256,256)
-        lb(sy,0,2)
-        lb(sy,2,2)
-        pool(0,4)
-        gw(0,512)
-        gs(0,256)
-        il(0,"s")
-        il(1,"s")
-        q(0)
-        mm(0,0,256,0)
-        q(1)
-        mm(1,0,256,1)
-        gsi(256,256,256,128,"w_raw128")
-        mm(0,256,128,2)
-        mm(1,256,128,3)
-        gsi(256,256,384,128,"w_raw128")
-        mm(0,384,128,4)
-        mm(1,384,128,5)
-        il(2,"s")
-        il(3,"gc")
-        q(2)
-        q(3)
-        mm(2,0,256,6)
-        mm(2,256,256,7)
-        si(0,0,256,0)
-        rd(0,0,256)
-        si(1,0,256,1)
-        rd(1,0,256)
-        mm(3,0,256,0)
-        mm(3,256,128,1)
-        room(0,256,256)
-        room(1,256,256)
-        si(0,256,128,2)
-        mm(3,384,128,2)
-        si(1,256,128,3)
-        si(0,384,128,4)
-        rd(0,256,256)
-        si(1,384,128,5)
-        rd(1,256,256)
-        st(0,2)
-        si(2,0,256,6)
-        si(2,256,256,7)
-        rd(2,0,256)
-        rd(2,256,256)
-        st(2)
-        si(3,0,256,0)
-        si(3,256,128,1)
-        si(3,384,128,2)
-        rd(3,0,256)
-        rd(3,256,128)
-        rd(3,384,128)
-        st(3)
+        last_runs = ((0, HALF), (HALF, QUARTER), (HALF + QUARTER, QUARTER))
+        for first, count in last_runs:
+            activate(3, first, count)
+        for first, count in last_runs:
+            take_maxima(3, first, count)
+        store(3, 1)

@@ -47,7 +47,7 @@ def tile_picked_pool_lin_silu_sub_p_kernel(tc, x_words, x_scales, w, b, offs, ou
         nc.vector.memset(scale_table[:], 0)
         nc.sync.dma_start(offsets[:], offs)
         nc.sync.dma_start(word_table[:], x_words[0].rearrange("p c r -> p (c r)").bitcast(I32))
-        load_scale_rows(nc.scalar, 2)
+        load_scale_rows(nc.scalar, 1)
         load_scale_rows(nc.scalar, 3)
 
         warm_in = keep.tile([P, 8], F32, name="warm_in")
@@ -56,7 +56,7 @@ def tile_picked_pool_lin_silu_sub_p_kernel(tc, x_words, x_scales, w, b, offs, ou
         nc.scalar.activation(warm_out[:], warm_in[:], SILU)
 
         load_scale_rows(nc.sync, 0)
-        load_scale_rows(nc.sync, 1)
+        load_scale_rows(nc.sync, 2)
 
         w_rows = w.rearrange("(p j) n -> p j n", j=PACK)
         w_raw = []

@@ -67,10 +67,10 @@ def tile_picked_pool_lin_silu_sub_p_kernel(tc, x_words, x_scales, w, b, offs, ou
 
         bias = []
         for first in (0, 2):
-            pair = keep.tile([P, 2], F32, name="bias%d" % first)
+            pair = keep.tile([P, 2, 8], F32, name="bias%d" % first)
             with nc.allow_non_contiguous_dma(reason="one bias value a partition and channel tile"):
-                nc.sync.dma_start(pair[:], b.rearrange("(t p) o -> p (t o)", p=P)[:, first : first + 2])
-            bias.extend(pair[:, u : u + 1] for u in range(2))
+                nc.sync.dma_start(pair[:, :, 0:1], b.rearrange("(t p) o -> p t o", p=P)[:, first : first + 2, :])
+            bias.extend(pair[:, u, 0:1] for u in range(2))
 
         pooled = aligned([P, 4 * V], F32, "pooled")
 

from contextlib import ExitStack

import concourse.mybir as mybir

K, T, D, S, V, N = 512, 1024, 8, 512, 64, 512
FLOPS = 2 * K * S * N

F32 = mybir.dt.float32
BF16 = mybir.dt.bfloat16
I32 = mybir.dt.int32
U32 = mybir.dt.uint32
U16 = mybir.dt.uint16
U8 = mybir.dt.uint8
FP8X4 = mybir.dt.float8_e4m3fn_x4
SILU = mybir.ActivationFunctionType.Silu
MAX = mybir.AluOpType.max
MULT = mybir.AluOpType.mult
ADD = mybir.AluOpType.add

P = 128
PACK = 4
QUADRANT = 32
PER_COLUMN = 16
BANK = 512
ALIGN = 256
HALF = S // 2
QUARTER = S // 4


def tile_picked_pool_lin_silu_sub_p_kernel(tc, x_words, x_scales, w, b, offs, out):
    nc = tc.nc
    with ExitStack() as ctx:
        keep = ctx.enter_context(tc.tile_pool(name="keep", bufs=1))
        psum = ctx.enter_context(tc.psum_pool(name="psum", bufs=1))

        def aligned(shape, dtype, name, tag=None):
            return keep.tile(shape, dtype, name=name, tag=tag or name, align_bytes=ALIGN)

        offsets = keep.tile([P, S // PER_COLUMN], U16, name="offsets")
        word_table = aligned([P, T], I32, "word_table")
        scale_table = aligned([P, T // 4], I32, "scale_table")

        def load_scale_rows(queue, quadrant):
            rows = x_scales[0].bitcast(I32)[PACK * quadrant : PACK * (quadrant + 1), :]
            queue.dma_start(scale_table[QUADRANT * quadrant : QUADRANT * quadrant + PACK, :], rows)

        nc.vector.memset(scale_table[:], 0)
        nc.sync.dma_start(offsets[:], offs)
        nc.sync.dma_start(word_table[:], x_words[0].rearrange("p c r -> p (c r)").bitcast(I32))
        load_scale_rows(nc.scalar, 1)
        load_scale_rows(nc.scalar, 3)

        warm_in = keep.tile([P, 8], F32, name="warm_in")
        warm_out = keep.tile([P, 8], F32, name="warm_out")
        nc.vector.memset(warm_in[:], 0.0)
        nc.scalar.activation(warm_out[:], warm_in[:], SILU)

        load_scale_rows(nc.sync, 0)
        load_scale_rows(nc.sync, 2)

        w_rows = w.rearrange("(p j) n -> p j n", j=PACK)
        w_raw = []
        for first, count in ((0, 1), (1, 1), (2, 2)):
            chunk = aligned([P, PACK, count * P], F32, "w_raw%d" % (first * P))
            nc.sync.dma_start(chunk[:], w_rows[:, :, first * P : (first + count) * P])
            w_raw.extend(chunk[:, :, u * P : (u + 1) * P] for u in range(count))

        bias = []
        for first in (0, 2):
            pair = keep.tile([P, 2, 8], F32, name="bias%d" % first)
            with nc.allow_non_contiguous_dma(reason="one bias value a partition and channel tile"):
                nc.sync.dma_start(pair[:, :, 0:1], b.rearrange("(t p) o -> p t o", p=P)[:, first : first + 2, :])
            bias.extend(pair[:, u, 0:1] for u in range(2))

        pooled = aligned([P, 4 * V], F32, "pooled")

        def gather(dst, table, first, count):
            entries = offsets[:, first // PER_COLUMN : (first + count) // PER_COLUMN]
            nc.vector.tensor_copy(dst, table.indirect(entries))

        grouped, w_codes, w_scales, sums, acts = {}, {}, {}, {}, {}

        def interleave_on_scalar(t):
            grouped[t] = aligned([P, P, PACK], BF16, "grouped%d" % t)
            nc.scalar.copy(
                grouped[t][:].rearrange("p (c i) j -> p c j i", i=4),
                w_raw[t].rearrange("p j (c i) -> p c j i", i=4),
            )

        def interleave_on_gpsimd(t):
            grouped[t] = aligned([P, P, PACK], BF16, "grouped%d" % t)
            nc.gpsimd.tensor_scalar(grouped[t][:], w_raw[t].rearrange("p j c -> p c j"), 1.0, 0.0, MULT, ADD)

        def quantize(t):
            w_codes[t] = aligned([P, P], U32, "w_codes%d" % t)
            w_scales[t] = aligned([P, P], U8, "w_scales%d" % t)
            nc.vector.quantize_mx(
                out=w_codes[t][:].bitcast(FP8X4),
                scales=w_scales[t][:],
                in_=grouped[t][:].rearrange("p c j -> p (c j)"),
            )

        def multiply(t, first, count, bank):
            sums[t, first] = psum.tile([P, BANK], F32, name="sums%d_%d" % (t, first), tag="bank%d" % bank)
            nc.tensor.matmul_mx(
                out=sums[t, first][:, 0:count],
                lhsT=w_codes[t][:].bitcast(FP8X4),
                lhsT_scale=w_scales[t][:],
                rhs=words[:, first : first + count].bitcast(FP8X4),
                rhs_scale=scales[first // HALF][:, first % HALF : first % HALF + count],
                start=True,
                stop=True,
            )

        def make_room(t, first, count):
            tile = aligned([P, count], F32, "act%d_%d" % (t, first))
            for start in range(first, first + count, QUARTER):
                acts[t, start] = tile[:, start - first : count]

        def activate(t, first, count):
            if (t, first) not in acts:
                make_room(t, first, count)
            nc.scalar.activation(acts[t, first][:, 0:count], sums[t, first][:, 0:count], SILU, bias=bias[t])

        def take_maxima(t, first, count):
            nc.vector.tensor_reduce(
                pooled[:, t * V + first // D : t * V + (first + count) // D],
                acts[t, first][:, 0:count].rearrange("p (v d) -> p v d", d=D),
                mybir.AxisListType.X,
                MAX,
            )

        def store(t, tiles):
            nc.sync.dma_start(
                out.rearrange("(t p) v -> p t v", p=P)[:, t : t + tiles, :],
                pooled[:, t * V : (t + tiles) * V].rearrange("p (t v) -> p t v", v=V),
            )

        scale_bytes = scale_table[:].bitcast(U8)
        words = aligned([P, S], U32, "words")
        gather(words[:], word_table[:].bitcast(U32), 0, S)
        scales = [aligned([P, HALF], U8, "scales0")]
        gather(scales[0][:], scale_bytes, 0, HALF)
        for t in (0, 1):
            interleave_on_scalar(t)
        for t in (0, 1):
            quantize(t)
            multiply(t, 0, HALF, bank=t)

        scales.append(aligned([P, HALF], U8, "scales1", tag="w_raw%d" % P))
        for quarter in (0, 1):
            first = HALF + quarter * QUARTER
            gather(scales[1][:, quarter * QUARTER : (quarter + 1) * QUARTER], scale_bytes, first, QUARTER)
            for t in (0, 1):
                multiply(t, first, QUARTER, bank=2 + 2 * quarter + t)

        interleave_on_scalar(2)
        interleave_on_gpsimd(3)
        quantize(2)
        quantize(3)
        for half in (0, 1):
            multiply(2, half * HALF, HALF, bank=6 + half)

        for t in (0, 1):
            activate(t, 0, HALF)
            take_maxima(t, 0, HALF)
        multiply(3, 0, HALF, bank=0)
        multiply(3, HALF, QUARTER, bank=1)
        for t in (0, 1):
            make_room(t, HALF, HALF)
        activate(0, HALF, QUARTER)
        multiply(3, HALF + QUARTER, QUARTER, bank=2)
        activate(1, HALF, QUARTER)
        for t in (0, 1):
            activate(t, HALF + QUARTER, QUARTER)
            take_maxima(t, HALF, HALF)
        store(0, 2)

        for half in (0, 1):
            activate(2, half * HALF, HALF)
        for half in (0, 1):
            take_maxima(2, half * HALF, HALF)
        store(2, 1)

        last_runs = ((0, HALF), (HALF, QUARTER), (HALF + QUARTER, QUARTER))
        for first, count in last_runs:
            activate(3, first, count)
        for first, count in last_runs:
            take_maxima(3, first, count)
        store(3, 1)
